import numpy as np, ml_dtypes
CORES = [242,247,114,119]
N = 4
BF = ml_dtypes.bfloat16
P, TW, M, RO = 2048, 2048, 3, 5
def parts(rng):
    v = rng.integers(0, 128, (N, 8, 16, P)); v[:, :, 15] = rng.integers(0, 2, (N, 8, P))
    t = rng.integers(0, 128, (N, 8, 16, TW)); t[:, :, 15] = rng.integers(0, 2, (N, 8, TW))
    return v, t, rng.integers(1, 256, (N, 8, 16)), rng.integers(0, 2048, (N, 8, RO, M))
def pack(v, t, w, k):
    return {"x": v.reshape(N, 128, P).astype(np.float32).astype(BF), "tm": t.reshape(N, 128, TW).astype(np.float32).astype(BF),
            "wt": np.ascontiguousarray(w.reshape(N, 128, 1)).astype(np.int32),
            "km": np.repeat(k.reshape(N, 8, 1, RO * M), 16, axis=2).reshape(N, 128, RO * M).astype(np.int32)}
def aim(rng, q, noth):
    u = np.arange(1, 4096, 2); i = u.copy()
    for _ in range(4): i = (i * (2 - u * i)) & 4095
    kk = ((q - (u * u >> 5)) * i) & (P - 1)
    ok = np.flatnonzero((kk < 2048) & (((u * u >> 4) & (TW - 1)) != noth))
    s = int(rng.choice(ok)); return int(u[s]), int(kk[s])
def column(rng, w, u, s):
    c = rng.integers(0, 128, 16); c[15] = s; c[:2] = 0
    z = (u - int(np.sum(w * c))) & 4095; c[0] = z & 63; c[1] = z >> 6
    return c
def setup_inputs(rng):
    return pack(*parts(rng))
def setup_inputs_ends(rng):
    v, t, w, k = parts(rng); w[:, :, 0] = 1; w[:, :, 1] = 64; w[:, :, 15] = 0
    for r in range(N):
        o = (r + 1) % N
        for g in range(8):
            case = (g - r) % 9
            a = int(rng.integers(1, P // 4)); b = int(rng.integers(P // 2, 3 * P // 4))
            if case < 2: a, b = 0, P - 1
            if case in (2, 3): b = a + 1
            if case == 8: a, b = int(rng.integers(1, P // 8)), int(rng.integers(7 * P // 8, P - 8))
            p, q = a, b
            if case == 7 or (case < 6 and rng.random() < 0.5): p, q = b, a
            s = int(rng.integers(0, 2)); u, k[r, g, 0, 0] = aim(rng, q, -1); c = column(rng, w[r, g], u, s); h = (u * u >> 4) & (TW - 1)
            if case == 4: v[r, g, 15] = s
            v[r, g, :, p] = c; v[r, g, :, q] = c
            if case in (0, 3): v[r, g, 15, q] = 1 - s
            t[o, g, :15, h] = c[:15]
            if case == 6: v[r, g, :, int(rng.integers(a + 1, b))] = c
            if case == 7: v[r, g, :, b + 3] = c
            if case in (1, 4, 5, 7, 8):
                p2, q2 = {1: (P // 3, P // 2), 4: (a + 1, P - 1), 5: (b - 1, b + 1), 7: (a + 2, b - 2), 8: (P // 2, P - 3)}[case]
                if (case == 4 and r % 2 == 0) or rng.random() < 0.5: p2, q2 = q2, p2
                u2, k[r, g, 0, 1] = aim(rng, q2, h); c2 = column(rng, w[r, g], u2, s if case == 4 else int(rng.integers(0, 2))); h2 = (u2 * u2 >> 4) & (TW - 1)
                v[r, g, :, p2] = c2; v[r, g, :, q2] = c2; t[o, g, :15, h2] = c2[:15]; t[o, g, 0, h2] = c2[0] ^ (2 if case == 8 else 1)
            if case == 8:
                ks = np.arange(2048); zs = ((u * u >> 5) + ks * u) & (P - 1)
                ks = ks[(zs > a) & (zs < b) & (zs != P // 2)]
                k[r, g, 0, 2] = int(rng.choice(ks)); z = ((u * u >> 5) + int(k[r, g, 0, 2]) * u) & (P - 1)
                cz = c.copy(); cz[0] = c[0] ^ 1; uz = (u + int(cz[0]) - int(c[0])) & 4095
                v[r, g, :, z] = cz; t[o, g, :15, (u * uz >> 4) & (TW - 1)] = c[:15]
    return pack(v, t, w, k)
def setup_inputs_kinds(rng):
    v, t, w, k = parts(rng); w[:] = w[:1].copy(); w[:, :, 15] = 0
    for g in (0, 2, 4):
        w[:, g, 0] = 1; w[:, g, 1] = 64; w[:, g, (2 if g == 2 else 8):] = 0
        u = 3 if g == 4 else 2 * int(rng.integers(0, 2048)) + 1; c = column(rng, w[0, g], u, 0)
        if g != 2: v[:, g, :8] = c[:8, None]
        else:
            v[:, g, :2] = c[:2, None]; v[:, g, 2:15] = rng.integers(0, 41, (N, 13, P)); k[:, g, 0] = k[:, g, 0, :1].copy()
            for r in range(N): v[r, g, 2:15, ((u * u >> 5) + int(k[r, g, 0, 0]) * u) & (P - 1)] = rng.integers(120, 128, 13)
    for g in (1, 3, 5, 6, 7):
        n = 5 if g % 2 else int(rng.integers(2, 6)); kd = rng.integers(0, 128, (16, n))
        if g % 2:
            kd[:, 4] = rng.integers(40, 88, 16)
            kd[:, :4] = kd[:, 4:] + rng.integers(8, 41, (16, 4)) * (2 * rng.integers(0, 2, (16, 4)) - 1)
        for r in range(N):
            kind = rng.integers(0, n, P)
            if g % 2:
                c = r % 4; uc, u4 = [int(np.sum(w[r, g] * kd[:, i])) & 4095 for i in (c, 4)]
                kind[((u4 * u4 >> 5) + k[r, g, 0] * u4) & (P - 1)] = c
                t[(r + 1) % N, g, :15, (uc * u4 >> 4) & (TW - 1)] = (kd[:15, c] + kd[:15, 4]) >> 1
            v[r, g] = kd[:, kind]
    v[:, :, 15] = rng.integers(0, 2, (N, 8, P))
    return pack(v, t, w, k)
def setup_inputs_void(rng):
    v, t, w, k = parts(rng); w[:, :, 0] = 1; w[:, :, 1] = 64; k[:, ::2] = k[:, ::2, :1, :1].copy()
    for g in (0, 6):
        v[:, g, 2:15] &= 3; t[:, g, :15] = 124 + (t[:, g, :15] & 3)
    us = np.arange(4096); j = np.arange(P)
    for r in range(N):
        for g in range(8):
            pre = np.full(P, -1); pre[((us * us >> 5) + int(k[r, g, 0, 0]) * us) & (P - 1)] = us
            z = (pre - np.sum(w[r, g, 2:, None] * v[r, g, 2:], axis=0)) & 4095
            v[r, g, 0] = np.where(pre >= 0, z & 63, v[r, g, 0]); v[r, g, 1] = np.where(pre >= 0, z >> 6, v[r, g, 1])
            if g in (0, 6):
                u = np.sum(w[r, g, :, None] * v[r, g], axis=0) & 4095; q = ((u * u >> 5) + int(k[r, g, 0, 0]) * u) & (P - 1)
                h = (u * u[q] >> 4) & (TW - 1); free = np.flatnonzero((q == j) & ~np.isin(h, h[q != j]))
                if len(free):
                    p = int(rng.choice(free)); t[(r + 1) % N, g, :15, int(h[p])] = v[r, g, :15, p]
    return pack(v, t, w, k)
def setup_inputs_small(rng):
    v, t, w, k = parts(rng)
    return pack(v & 1, t & 1, w, k)
def setup_inputs_spread(rng):
    v, t, w, k = parts(rng); both = []
    for a in (v, t):
        n = a.shape[-1]; b = np.minimum((np.exp2(8 * rng.random((N, 8, 1, n))) * rng.random(a.shape)).astype(np.int64), 127)
        z = rng.integers(0, 32, (N, 8, 1, n)); b = np.where(z == 0, 0, np.where(z == 1, 127, b)); b[:, :, 15] = a[:, :, 15]; both.append(b)
    w = np.minimum(np.exp2(8.1 * rng.random((N, 8, 16))).astype(np.int64), 255); w[:, :, 3] = 0; w[:, :, 4] = 255
    w[:, 5] = rng.integers(200, 256, (N, 16)); w[:, 6] = 255
    both[0][:, 5, :15] = rng.integers(100, 128, (N, 15, P)); both[0][:, 6, :15] = rng.integers(64, 128, (N, 15, P))
    both[0][:, 6, :15, P - 1] = 127; both[0][:, 6, 15, P - 1] = 1
    k = np.minimum(np.exp2(11.1 * rng.random((N, 8, RO, M))).astype(np.int64) - 1, 2047); k[:, 1, 0, 0] = 0; k[:, 2, 0, 1] = 2047
    return pack(both[0], both[1], w, k)
def check_inputs(d):
    bad = []
    for name in ("x", "tm"):
        a = np.asarray(d[name]).astype(np.float32)
        if not np.all((a >= 0) & (a <= 127) & (np.floor(a) == a)): bad.append("whole numbers of " + name)
        if not np.all(a[:, 15::16] <= 1): bad.append("signs of " + name)
    for name, hi in (("wt", 255), ("km", 2047)):
        if np.min(d[name]) < 0 or np.max(d[name]) > hi: bad.append("range of " + name)
    a = np.asarray(d["km"]); a = a.reshape(a.shape[0], 8, 16, -1)
    if not np.all(a == a[:, :, :1]): bad.append("rows of km alike")
    return bad
def reference(x, tm, wt, km):
    v = x.astype(np.float32).astype(np.int32).reshape(N, 8, 16, P); tp = tm.astype(np.float32).astype(np.int32).reshape(N, 8, 16, TW)
    w = wt.astype(np.int32).reshape(N, 8, 16, 1); k = km.astype(np.int32).reshape(N, 8, 16, RO, M)[:, :, 0]; j = np.arange(P)
    for t in range(RO):
        u = np.add.reduce(w * v, axis=2, dtype=np.int32) & 4095
        bq = bd = None
        for m in range(M):
            q = ((u * u >> 5) + k[:, :, t, m][:, :, None] * u) & (P - 1)
            xq = np.take_along_axis(v, q[:, :, None, :], 3)
            dm = np.where(q == j, 8192, np.add.reduce(np.abs(v - xq)[:, :, :15], axis=2))
            if m == 0: bq, bd = q, dm
            else: bq, bd = np.where(dm < bd, q, bq), np.minimum(bd, dm)
        xq = np.take_along_axis(v, bq[:, :, None, :], 3)
        h = (u * np.take_along_axis(u, bq, 2) >> 4) & (TW - 1)
        got = np.stack([np.take_along_axis(tp[(r + 1 + t % (N - 1)) % N], h[r][:, None, :], 2) for r in range(N)])
        e = bd + np.add.reduce(np.abs(v + xq - 2 * got)[:, :, :15], axis=2)
        alike = v[:, :, 15] == xq[:, :, 15]; lo = np.minimum(j, bq); hi = np.maximum(j, bq)
        nv = np.empty_like(v)
        for r in range(N):
            for g in range(8):
                p = int(np.argmin(e[r, g])); a, b = int(lo[r, g, p]), int(hi[r, g, p])
                z = v[r, g].copy(); z[:15, a] = (v[r, g, :15, a] + v[r, g, :15, b]) >> 1
                tp[r, g, :, int(h[r, g, p])] = z[:, a]
                if not alike[r, g, p]:
                    z[:, a + 1:b + 1] = z[:, a + 1:b + 1][:, ::-1].copy(); z[15, a + 1:b + 1] = 1 - z[15, a + 1:b + 1]
                else:
                    c, d = b, P - 1
                    inside = alike[r, g] & (lo[r, g] > a) & (lo[r, g] < b)
                    if np.any(inside):
                        p2 = int(np.argmin(np.where(inside, e[r, g], 2 ** 20)))
                        if hi[r, g, p2] > b: c, d = int(lo[r, g, p2]), int(hi[r, g, p2])
                    z = z[:, np.concatenate([j[:a + 1], j[b + 1:d + 1], j[c + 1:b + 1], j[a + 1:c + 1], j[d + 1:]])]
                nv[r, g] = z
        v = nv
    return {"y": v.reshape(N, 128, P).astype(np.float32).astype(BF)}

@@ -1,0 +1,501 @@
+from concourse.bass import DstId, RemoteDMATransfer
+from concourse.mybir import AluOpType, AxisListType, ActivationFunctionType
+
+OP, AF = AluOpType, ActivationFunctionType
+P, TW, M, RO, NR = 2048, 2048, 3, 5, 4
+NC = P // 16
+CH = [(0, 64), (64, 64)]
+SM = [0]
+SPL = [0, 1]
+SELF_D = 1920
+SPX = 2 * P
+BIG = float(2 ** 24)
+SENDS = {0: (1, 2, 3), 1: (1, 2, 3), 2: (1, 2), 3: (2,)}
+CY, GA, FIX, WAKE = .00083, 1.5, .03, .08
+PE, BON, LATE = [.0006], 1.0, 7.0
+
+SCRATCH = {}
+for _d, _l in {
+    "float32": "idnf 128 nf 128 xf 2048 cf 32 kmf 16 grp 128 m16 16 emn 128 nt 128 nt8 128 ntm 128 pt 128 v3 128 vmn 128 b4 128 bq 128 "
+               "lo 128 key 128 lod 128 prd 128 prh 128 prk 128 k2a 128 k2 128 rn 128 bs 128 y1 128 g2 128 sf 128 nb2 128 dg 16 dg2 16 "
+               "c 64 nc 16 upd 64 land 192",
+    "bfloat16": "xa 4112 xb 4112 tmo 2048 tb1 2064 tb2 2064 tb3 2064 xq 2048 ag 2048 az 2048 yb 2048 bm 2048 wb 2048 mf 2048 mz 2048 "
+                "xs 2048 as 2048 idm 128 ma 128 mb 128 idn 128 idf 128 idj 128 idk 128 ids 128 idc 128 id1 128 id2 128 em 128 one 64 "
+                "eqb 384 sg 128 nd 16",
+    "float16": "mn 6144 md 2048 q16 384 id16 128",
+    "int32": "io2 2048 ic 128 ipart 4 ci 16 wti 4 kmi 16 tmpi 128 tmpj 128 ui 128 u 128 sq 128 s5 128 t3 384 q3 384 vm 128 qs 128 b1 128 "
+             "ri 128 uq 128 hp 128 hs 128 ki 128 kv 128 cii 16",
+    "uint16": "l3 384 lq 128 lh 128 ls 128 l1 16"}.items():
+    _w = _l.split()
+    for _i in range(0, len(_w), 2):
+        SCRATCH[_w[_i]] = ("sbuf", [128, int(_w[_i + 1])], _d)
+PSUMS = ["ps0", "ps1", "ps2", "ps3", "ps5", "z0", "z1", "z2"]
+for _n in PSUMS:
+    SCRATCH[_n] = ("psum", [128, 512], "float32")
+SEMAPHORES = ["qv", "qs", "qp", "qg", "dx0", "dx1", "dw", "dk", "dt", "dy0", "dy1", "dy2", "dy3", "ls", "tma1", "tma2", "tma3"] + \
+             ["ua%d_%d" % (t, o) for t in SENDS for o in SENDS[t]]
+
+
+def rank_program(g, core, T, topo):
+    rank, cores = T.rank_of(core), T.cores
+    if rank is None:
+        return
+    Q = {"v": g.vector, "s": g.scalar, "p": g.tensor, "g": g, "y": g.sync}
+    QS = {"v": "qv", "s": "qs", "p": "qp", "g": "qg"}
+    ops, wr, rd, bon = [], {}, {}, [0.0]
+
+    def A(n, a=0, b=None, st=1):
+        b = T[n].shape[-1] if b is None else b
+        return (T[n][:, a:b] if st == 1 else T[n][:, a:b:st], [(n, a, b)], (b - a + st - 1) // st)
+
+    def IND(w, o):
+        return (w[0].indirect(o[0]), w[1] + o[1], -16 * o[2])
+
+    def note(q, fn, outs, ins, cost, sem="", inc=1, lat=0.0, ev=None, after=()):
+        me, pre = len(ops), set(after)
+        R = [(r, 0) for o in ins for r in o[1]] + [(r, 1) for o in outs for r in o[1]]
+        for (n, a, b), k in R:
+            for d, w2 in ((wr, 1), (rd, 0)):
+                for a2, b2, q2, i2 in d.setdefault(n, []):
+                    if (n in PSUMS and q2 != q) or (a < b2 and a2 < b and (k or w2)):
+                        pre.add(i2)
+        for (n, a, b), k in R:
+            if k and n not in PSUMS:
+                for d in (wr, rd):
+                    d[n] = [x for x in d[n] if not (a <= x[0] and x[1] <= b)]
+            (wr if k else rd)[n].append((a, b, q, me))
+        pre.discard(me)
+        ops.append(dict(q=q, fn=fn, pre=sorted(pre), cost=cost, bon=bon[0], sem=sem, inc=inc, lat=lat, ev=ev))
+        return me
+
+    def vcost(o, ins, two=False, half=False):
+        n = max([x[2] for x in ins] + [o[2]])
+        for x in ins + [o]:
+            if x[2] < 0: return -x[2] * CY * (GA if x is not o else 3) + FIX + .05
+        ps = any(x[1][0][0] in PSUMS for x in ins)
+        if two and not ps: n *= 2
+        if half and not ps and all(SCRATCH.get(x[1][0][0], ("", "", ""))[2] in ("bfloat16", "float16", "uint16") for x in ins + [o]): n //= 2
+        return max(64, n) * CY + FIX
+
+    def TT(o, x, y, op):
+        note("v", lambda: g.vector.tensor_tensor(o[0], x[0], y[0], op), [o], [x, y], vcost(o, [x, y], two=True))
+
+    def TS(o, x, s1, op0, s2=None, op1=None):
+        ins = [x] + [s for s in (s1, s2) if isinstance(s, tuple)]
+        v1 = s1[0] if isinstance(s1, tuple) else s1
+        v2 = s2[0] if isinstance(s2, tuple) else s2
+        if op1 is None:
+            note("v", lambda: g.vector.tensor_scalar(o[0], x[0], v1, None, op0), [o], ins, vcost(o, [x], half=True))
+        else:
+            note("v", lambda: g.vector.tensor_scalar(o[0], x[0], v1, v2, op0, op1), [o], ins, vcost(o, [x], half=True))
+
+    def CP(o, x):
+        note("v", lambda: g.vector.tensor_copy(o[0], x[0]), [o], [x], vcost(o, [x], half=True))
+
+    def RED(o, x, op):
+        note("v", lambda: g.vector.tensor_reduce(o[0], x[0], AxisListType.X, op), [o], [x], vcost(o, [x]))
+
+    def FILL(o, v):
+        note("v", lambda: g.vector.memset(o[0], v), [o], [], vcost(o, []))
+
+    def ACT(o, x, func=AF.Copy, bias=None, scale=None):
+        kw = {}
+        if bias is not None: kw["bias"] = bias[0]
+        if scale is not None: kw["scale"] = scale[0] if isinstance(scale, tuple) else scale
+        note("s", lambda: g.scalar.activation(o[0], x[0], func, **kw), [o],
+             [x] + [s for s in (bias, scale) if isinstance(s, tuple)], vcost(o, [x]) + .015)
+
+    def MM(o, pairs, start=True, stop=True):
+        def go():
+            for i, z in enumerate(pairs):
+                k = g.tensor.matmul((z[2] if len(z) > 2 else o)[0], z[0][0], z[1][0], start and i == 0, stop and i == len(pairs) - 1)
+            return k
+        f = [max(64, z[1][2]) * PE[0] * (4 if SCRATCH[z[0][1][0][0]][2] == "float32" else 1) for z in pairs]
+        note("p", go, [o], [y for z in pairs for y in z[:2]], sum(f), lat=.06)
+
+    def DMA(q, o, x, sem):
+        note(q, lambda: Q[q].dma_start(o[0], x[0]), [o], [x], .1, sem, 16, 4.0)
+
+    def SUMS(mat, buf, base, n):
+        return [(A(mat, jj * 128, jj * 128 + 128), A(buf, base + jj, base + 16 * n, 16)) for jj in range(16)]
+
+    def IOTA(pattern, b, cm, base=0):
+        note("g", lambda: g.iota(b[0], pattern, base, cm), [b], [], .13 + 2 * b[2] * CY)
+
+    def H(ap):
+        return (ap, [], 0)
+
+    DMA("y", A("wti", 0, 1), H(T.wt[:]), "dw")
+    DMA("y", A("xa", 0, P // 2), H(T.x[:, 0:P // 2]), "dx0")
+    DMA("s", A("tmo"), H(T.tm[:]), "dt")
+    DMA("y", A("xa", P // 2, P), H(T.x[:, P // 2:P]), "dx1")
+    DMA("y", A("kmi", 0, 15), H(T.km[:]), "dk")
+
+    IOTA([[0, 1]], A("ipart", 0, 1), 1)
+    IOTA([[1, 128]], A("ic"), 0)
+    for k in (0, 1):
+        IOTA([[-1000, 8], [1, 8], [1000, 16]], A("io2", 1024 * k, 1024 * k + 1024), 0, -8000 * k)
+    C = lambda i: A("cf", i, i + 1)
+    (JJ, GK, IPF, F15, R15N, FIRST, NF, ODD, MH, SX, ST, CW, CMD, CMF, CMZ, CJ, CK, CB, CTH, CC2, C2047, C8K, CMH2, CQ, CP23, CM23, C1,
+     CM2047) = [C(i) for i in range(28)]
+    TS(A("ci", 0, 1), A("ipart", 0, 1), 15, OP.bitwise_and)
+    TS(A("ci", 1, 2), A("ipart", 0, 1), 4, OP.arith_shift_right)
+    TS(A("ci", 2, 3), A("ipart", 0, 1), 1, OP.bitwise_and)
+    CP(JJ, A("ci", 0, 1)); CP(GK, A("ci", 1, 2)); CP(ODD, A("ci", 2, 3)); CP(IPF, A("ipart", 0, 1))
+    TS(F15, JJ, 15.0, OP.is_lt)
+    TS(FIRST, JJ, 0.0, OP.is_equal)
+    TS(NF, JJ, 0.0, OP.is_gt)
+    CP(CW, A("wti", 0, 1))
+    TS(CMD, F15, -8192.0, OP.mult, -8192.0, OP.add)
+    TS(CMF, F15, 8192.0, OP.mult)
+    TS(CMZ, F15, 2047.0, OP.mult, 1.0, OP.add)
+    TS(CJ, F15, 2.0, OP.mult, -1.0, OP.add)
+    TS(CK, F15, -2.0, OP.mult)
+    TS(R15N, F15, 1.0, OP.mult, -1.0, OP.add)
+    TS(CB, R15N, -1.0, OP.mult)
+    TS(MH, F15, 0.5, OP.mult)
+    TS(CMH2, MH, -1.0, OP.mult, 1.0, OP.add)
+    TS(SX, JJ, float(SPX), OP.add, NF, OP.mult)
+    TS(ST, JJ, float(TW), OP.add, NF, OP.mult)
+    for b, v in ((CTH, -8192.0 * (SELF_D - 7)), (CC2, 1024.0 * SELF_D), (C2047, 2047.0), (C8K, 8192.0), (CQ, -0.25),
+                 (CP23, 8388608.0), (CM23, -8388608.0), (C1, 1.0), (CM2047, -2047.0)):
+        FILL(b, v)
+    TS(A("idn"), A("ic"), IPF, OP.is_equal)
+    TS(A("tmpi"), A("ic"), 4, OP.arith_shift_right)
+    TS(A("grp"), A("tmpi"), GK, OP.is_equal)
+    TS(A("tmpj"), A("ic"), 15, OP.bitwise_and)
+    TS(A("emn"), A("tmpj"), 15.0, OP.is_equal, F15, OP.mult)
+    TT(A("prd"), A("emn"), A("grp"), OP.mult)
+    TS(A("idf"), A("idn"), F15, OP.mult)
+    TT(A("em"), A("idf"), A("prd"), OP.subtract)
+    for k in (0, 1):
+        TS(A("wb", 1024 * k, 1024 * k + 1024), A("io2", 1024 * k, 1024 * k + 1024), GK, OP.is_equal, CW, OP.mult)
+    TS(A("md"), A("io2"), GK, OP.is_equal, CMD, OP.mult)
+    TS(A("bm"), A("io2"), GK, OP.is_equal)
+    ACT(A("mf"), A("bm"), AF.Copy, None, CMF)
+    ACT(A("mz"), A("bm"), AF.Copy, None, CMZ)
+    CP(A("kmf", 0, 15), A("kmi", 0, 15))
+    TS(A("nt"), A("ic"), 16.0, OP.mult, JJ, OP.add)
+    TS(A("nt8"), A("nt"), 8.0, OP.mult, -8192.0, OP.add)
+    TS(A("ntm"), A("nt"), -2047.0, OP.add)
+    PL = A("ps0", 0, 128)
+    CP(PL, A("nt"))
+    TS(A("idj"), A("idn"), CJ, OP.mult)
+    TS(A("idk"), A("idn"), CK, OP.mult)
+    TS(A("ids"), A("idn"), float(SELF_D * 8192), OP.mult)
+    TS(A("idc"), A("idn"), float(SELF_D * 1024), OP.mult)
+    TS(A("id1"), A("idn"), 2048.0, OP.mult)
+    TS(A("id2"), A("idn"), 4096.0, OP.mult)
+    TS(A("idm"), A("idn"), -1.0, OP.mult)
+    TS(A("id16"), A("ic"), IPF, OP.is_equal)
+    TS(A("idnf"), A("ic"), IPF, OP.is_equal)
+    TS(A("m16"), A("ic", 0, 16), JJ, OP.is_equal)
+    FILL(A("one"), 1.0); FILL(A("nd"), 0.0); FILL(A("upd"), 0.0)
+
+    sent, arrived = [0], {}
+
+    def send_table(o):
+        d = cores[(rank - o) % NR]
+        rid, pid = topo.addr(d, core)
+        sent[0] += len(topo.engines(core, d))
+        arrived["tma%d" % o] = len(topo.engines(cores[(rank + o) % NR], core))
+        k = note("g", lambda: g.remote_dma(T["tb%d" % o][:, 0:TW], T.tmo[:], T.sem["tma%d" % o], T.sem.ls, pid, rid, topo.mask(core, d)),
+                 [], [A("tmo")], .5, None)
+        note("x", None, [A("tb%d" % o, 0, TW)], [], 0, None, 1, 4.0 + 6 * o, ("tma%d" % o, arrived["tma%d" % o]), (k,))
+    for o in (1, 2, 3): send_table(o)
+
+    cc = lambda i: A("c", i, i + 1)
+    ii = lambda i: A("cii", i, i + 1)
+    seen, landed = set(), {}
+
+    def updates(t):
+        o = 1 + t % 3
+        for t0 in range(t):
+            if (t0, o) in landed and (t0, o) not in seen:
+                seen.add((t0, o))
+                k = landed[(t0, o)]
+                L = A("l1", 4 + 2 * (len(seen) % 2), 5 + 2 * (len(seen) % 2))
+                TS(L, A("land", 16 * k + 1, 16 * k + 2), FIRST, OP.mult, ST, OP.add)
+                CP(IND(A("tb%d" % o), L), A("land", 16 * k, 16 * k + 16))
+
+    def shares(r, t):
+        src, dst = cores[r], {o: cores[(r - o) % NR] for o in SENDS[t]}
+        away = [o for o in SENDS[t] if dst[o] not in topo.cores_of(src)]
+        off = topo.engines(src, dst[away[0]])
+        w = len(off) // len(away)
+        es = {o: off[i * w:i * w + w] for i, o in enumerate(away)}
+        for o in SENDS[t]:
+            if o not in es: es[o] = [e for e in topo.engines(src, dst[o]) if e not in off]
+        return es
+
+    def send_new(t):
+        es, xs = shares(rank, t), []
+        for o in SENDS[t]:
+            rid, pid = topo.addr(cores[(rank - o) % NR], core)
+            k = len(landed)
+            landed[(t, o)] = k
+            xs.append(RemoteDMATransfer(dst_ids=[DstId(rid=rid, pnc=pid)], dma_engine_mask=sum(1 << e for e in es[o]),
+                                        remote_sem=T.sem["ua%d_%d" % (t, o)], src=T.upd[:, 16 * t:16 * t + 16],
+                                        dst=T.land[:, 16 * k:16 * k + 16]))
+            sent[0] += len(es[o])
+            arrived["ua%d_%d" % (t, o)] = len(shares((rank + o) % NR, t)[o])
+        me = note("g", lambda: g.remote_dma_fused(xs, local_sem=T.sem.ls), [], [A("upd", 16 * t, 16 * t + 16)], .5, None)
+        for o in SENDS[t]:
+            k, s = landed[(t, o)], "ua%d_%d" % (t, o)
+            note("x", None, [A("land", 16 * k, 16 * k + 16)], [], 0, None, 1, LATE, (s, arrived[s]), (me,))
+
+    def one_round(t):
+        X, XN = ("xa", "xb") if t % 2 == 0 else ("xb", "xa")
+        TB = "tb%d" % (1 + t % 3)
+        MM(A("ps1", 0, 128), SUMS("wb", X, 0, NC))
+        for k in range(4):
+            b = A(["z2", "z0", "z1", "ps2"][k])
+            MM(b, [(A("em"), A(X, 512 * k, 512 * k + 512))])
+            ACT(A("xf", 512 * k, 512 * k + 512), b, AF.Identity, R15N)
+        for k in range(4):
+            ACT(A(X, P + 512 * k, P + 512 * k + 512), A(X, 512 * k, 512 * k + 512), AF.Identity, CB, CJ)
+        MM(A("ps5", 0, 128), SUMS("mf", X, 0, NC))
+        CP(A("ui"), A("ps1", 0, 128))
+        TS(A("u"), A("ui"), 4095, OP.bitwise_and)
+        TT(A("sq"), A("u"), A("u"), OP.mult)
+        TS(A("s5"), A("sq"), 5, OP.arith_shift_right)
+        for m in range(M):
+            a, b = 128 * m, 128 * m + 128
+            TS(A("ps0", a + 128, b + 128), A("u"), A("kmf", 3 * t + m, 3 * t + m + 1), OP.mult)
+            TT(A("t3", a, b), A("s5"), A("ps0", a + 128, b + 128), OP.add)
+            TS(A("q3", a, b), A("t3", a, b), P - 1, OP.bitwise_and)
+            CP(A("l3", a, b), A("q3", a, b))
+            TT(A("eqb", a, b), A("q3", a, b), PL, OP.is_equal)
+            CP(A("q16", a, b), A("q3", a, b))
+        ACT(A("nf"), A("ps5", 0, 128), AF.Identity, C8K, -1.0)
+        TT(A("pt"), A("nt8"), A("ps5", 0, 128), OP.add)
+
+        def pick(out, tab, lst, a, b, i):
+            for k, h in enumerate(range(a, b, 32)):
+                o, x = A(out, 16 * h, 16 * min(h + 32, b)), IND(A(tab, 0, P), A(lst, h, min(h + 32, b)))
+                if i in SPL and k % 2: CP(o, x)
+                else: ACT(o, x, AF.Copy)
+
+        def near(c, i):
+            c0, n = c
+            a = 16 * c0
+            e = lambda m: A("eqb", 128 * m + c0, 128 * m + c0 + n)
+            k = lambda m: A("q16", 128 * m + c0, 128 * m + c0 + n)
+            l = lambda m: A("l3", 128 * m + c0, 128 * m + c0 + n)
+            o0, o1 = A("ps2", 0, n), A("ps2", n, 2 * n)
+            for m in range(2 if i in SM else 3):
+                TT(A("mn", 3 * a + 16 * n * m, 3 * a + 16 * n * (m + 1)), IND(A("xf"), l(m)), A(X, a, a + 16 * n), OP.min)
+            MM(A("ps2", 0, 2 * n), SUMS("md", "mn", 48 * c0, 2 * n) +
+               [(A("ids"), e(0), o0), (A("ids"), e(1), o1), (A("id1"), A("one", 0, n), o1), (A("id16"), k(0), o0), (A("id16"), k(1), o1)])
+            last = [(A("ids"), e(2)), (A("id2"), A("one", 0, n)), (A("id16"), k(2))]
+            if i in SM:
+                for p0 in range(a, a + 16 * n, 512):
+                    p1 = min(p0 + 512, a + 16 * n)
+                    w = A("z2", 0, p1 - p0)
+                    ACT(A("xs", p0, p1), IND(A(X, 0, P), A("l3", 256 + p0 // 16, 256 + p1 // 16)), AF.Copy)
+                    MM(w, [(A("idm"), A(X, p0, p1)), (A("idn"), A("xs", p0, p1))])
+                    ACT(A("as", p0, p1), w, AF.Abs)
+                MM(A("ps3", 0, n), SUMS("mf", "as", a, n) + last + [(A("idnf"), A("nf", c0, c0 + n))])
+            else:
+                MM(A("ps3", 0, n), SUMS("md", "mn", 48 * c0 + 32 * n, n) + last)
+            ACT(A("v3", c0, c0 + n), o0, AF.Copy)
+            TT(A("vmn", c0, c0 + n), A("v3", c0, c0 + n), o1, OP.min)
+
+        def choose(c, i):
+            a, b, n = c[0], c[0] + c[1], c[1]
+            TT(A("vm", a, b), A("vmn", a, b), A("ps3", 0, n), OP.min)
+            TS(A("qs", a, b), A("vm", a, b), P - 1, OP.bitwise_and)
+            CP(A("lq", a, b), A("qs", a, b))
+            pick("xq", X, "lq", a, b, i)
+            MM(A("ps5", 128, 128 + n), SUMS("wb", "xq", 16 * a, n))
+            TS(A("b1", a, b), A("vm", a, b), -8192, OP.bitwise_and)
+            TT(A("b4", a, b), A("b1", a, b), A("pt", a, b), OP.add)
+            ACT(A("sg", a, b), A("b4", a, b), AF.Sign, CTH)
+            ACT(A("bq", a, b), A("b4", a, b), AF.Identity, CC2, 0.25)
+            TT(A("lo", a, b), A("qs", a, b), A("ps0", a, b), OP.min)
+
+        def asked(c, i):
+            a, b, n = c[0], c[0] + c[1], c[1]
+            CP(A("ri", a, b), A("ps5", 128, 128 + n))
+            TS(A("uq", a, b), A("ri", a, b), 4095, OP.bitwise_and)
+            TT(A("hp", a, b), A("uq", a, b), A("u", a, b), OP.mult)
+            TS(A("hs", a, b), A("hp", a, b), 4, OP.arith_shift_right, TW - 1, OP.bitwise_and)
+            CP(A("lh", a, b), A("hs", a, b))
+            sg = [(A("z%d" % (k % 2), 0, min(512, 16 * b - p0)), p0, min(p0 + 512, 16 * b)) for k, p0 in enumerate(range(16 * a, 16 * b, 512))]
+            for z, p0, p1 in sg:
+                MM(z, [(A("idj"), A(X, p0, p1)), (A("idn"), A("xq", p0, p1))], True, False)
+            pick("ag", TB, "lh", a, b, i)
+            for z, p0, p1 in sg:
+                MM(z, [(A("idk"), A("ag", p0, p1))], False, True)
+                ACT(A("az", p0, p1), z, AF.Abs)
+
+        def keyed(c):
+            a, b = c[0], c[0] + c[1]
+            MM(A("ps1", a, b), SUMS("mz", "az", 16 * a, c[1]) + [(A("idc"), A("sg", a, b))])
+            TT(A("key", a, b), A("bq", a, b), A("ps1", a, b), OP.add)
+
+        AC, BC, INV, NIN, BA, B1, B1I, RD, SL, BS, AB, RI = [cc(i) for i in range(10, 22)]
+        E0, E1, E2 = [A("ps0", 128 * m + 128, 128 * m + 256) for m in range(3)]
+        updates(t)
+        for i, c in enumerate(CH):
+            bon[0] = BON * (len(CH) - i)
+            near(c, i)
+            choose(c, i)
+            asked(c, i)
+        for i, c in enumerate(CH):
+            bon[0] = BON * (len(CH) - i)
+            keyed(c)
+            a, b = c[0], c[0] + c[1]
+            e = A("ps0", 128 + a, 128 + b)
+            CP(A("ki", a, b), A("key", a, b))
+            TS(A("kv", a, b), A("ki", a, b), 1, OP.bitwise_and)
+            TS(e, A("kv", a, b), -4096.0, OP.mult)
+            TT(A("lod", a, b), A("lo", a, b), e, OP.add)
+        bon[0] = 0.0
+
+        def lowest(src, out, dg):
+            RED(out, src, OP.min)
+            TS(A(dg), A("m16"), out, OP.mult)
+            MM(A("ps1", 0, 16), [(A("grp"), A(dg))])
+
+        lowest(A("key"), cc(0), "dg")
+        RED(cc(1), A("ps1", 0, 16), OP.min)
+        TS(E1, A("key"), cc(1), OP.is_equal)
+        TT(A("prd"), A("qs"), E1, OP.mult)
+        RED(cc(2), A("prd"), OP.add)
+        MM(A("ps1", 0, 1), [(A("grp"), cc(2))])
+        if t < RO - 1:
+            TT(A("prh"), A("hs"), E1, OP.mult)
+            RED(cc(27), A("prh"), OP.add)
+            MM(A("ps3", 64, 65), [(A("grp"), cc(27))])
+            CP(A("upd", 16 * t + 1, 16 * t + 2), A("ps3", 64, 65))
+        CP(ii(0), cc(1))
+        TS(ii(1), ii(0), 1, OP.arith_shift_right, P - 1, OP.bitwise_and)
+        TS(ii(2), ii(0), 1, OP.bitwise_and)
+        CP(INV, ii(2))
+        ACT(NIN, INV, AF.Identity, C1, -1.0)
+        TT(AC, ii(1), A("ps1", 0, 1), OP.min)
+        TT(BC, ii(1), A("ps1", 0, 1), OP.max)
+        TS(E0, A("lod"), AC, OP.is_le, BIG, OP.mult)
+        TT(A("k2a"), A("key"), E0, OP.max)
+        TS(E2, A("lod"), BC, OP.is_ge, BIG, OP.mult)
+        TT(A("k2"), A("k2a"), E2, OP.max)
+        lowest(A("k2"), cc(3), "dg2")
+        RED(cc(4), A("ps1", 0, 16), OP.min)
+        TS(E0, A("k2"), cc(4), OP.is_equal)
+        TT(A("prk"), A("qs"), E0, OP.mult)
+        RED(cc(5), A("prk"), OP.add)
+        MM(A("ps1", 0, 1), [(A("grp"), cc(5))])
+        CP(ii(4), cc(4))
+        TS(ii(5), ii(4), 1, OP.arith_shift_right, P - 1, OP.bitwise_and)
+        TS(cc(6), cc(4), BIG, OP.is_lt, NIN, OP.mult)
+        ACT(BA, AC, AF.Identity, BC, -1.0)
+        ACT(RD, BA, AF.Copy, None, NIN)
+        ACT(RI, INV, AF.Identity, RD, float(P + 1))
+        ACT(AB, AC, AF.Identity, BC)
+        ACT(BS, AB, AF.Identity, RI, INV)
+        ACT(SL, INV, AF.Copy, None, -2.0)
+        ACT(A("rn"), A("nt"), AF.Identity, BS, SL)
+        ACT(A("nb2"), A("ntm"), AF.Identity, BA)
+        ACT(B1, BC, AF.Identity, C2047, -1.0)
+        ACT(B1I, B1, AF.Copy, None, NIN)
+        ACT(cc(32), BC, AF.Identity, CM2047)
+        TS(A("l1", 0, 1), ODD, BA, OP.mult, AC, OP.add)
+        ACT(A("nc"), IND(A(X, 0, P), A("l1", 0, 1)), AF.Copy)
+        TS(A("l1", 2, 3), FIRST, AC, OP.mult, SX, OP.add)
+        ACT(cc(22), A("nc", 0, 1), AF.Identity, CQ, CMH2)
+        ACT(cc(28), A("nc", 1, 2), AF.Identity, cc(22), MH)
+        ACT(cc(29), cc(28), AF.Identity, CP23)
+        ACT(A("nd", 0, 1), cc(29), AF.Identity, CM23)
+        CP(IND(A(X), A("l1", 2, 3)), A("nd"))
+        if t < RO - 1:
+            ACT(A("upd", 16 * t, 16 * t + 1), A("nd", 0, 1), AF.Copy)
+            send_new(t)
+        ACT(cc(30), AC, AF.Copy, None, -1.0)
+        ACT(cc(31), BC, AF.Copy, None, -1.0)
+        ACT(A("ma"), A("nt"), AF.Sign, cc(30))
+        ACT(A("mb"), A("nt"), AF.Sign, cc(31))
+        ACT(A("ma"), A("ma"), AF.Relu)
+        ACT(A("mb"), A("mb"), AF.Relu, None, INV)
+        MM(A("z0", 0, 128), [(A("idn"), A("ma")), (A("idm"), A("mb"))])
+        TT(E2, A("rn"), A("z0", 0, 128), OP.mult)
+        TT(A("bs"), A("nt"), E2, OP.add)
+        TT(cc(8), ii(5), A("ps1", 0, 1), OP.max)
+        TT(cc(7), ii(5), A("ps1", 0, 1), OP.min)
+        TS(cc(9), cc(8), BC, OP.is_gt, cc(6), OP.mult)
+        TT(cc(23), cc(8), cc(7), OP.subtract)
+        TS(cc(25), cc(23), cc(32), OP.add, cc(9), OP.mult)
+        TS(cc(24), cc(8), 2047.0, OP.subtract, cc(9), OP.mult)
+        TT(cc(26), cc(25), B1I, OP.add)
+        TS(E0, A("nb2"), cc(25), OP.is_gt, RD, OP.mult)
+        TT(A("y1"), A("bs"), E0, OP.subtract)
+        TS(E2, A("ntm"), cc(24), OP.is_gt, cc(26), OP.mult)
+        TS(A("g2"), A("nb2"), cc(24), OP.is_gt, cc(26), OP.mult)
+        TT(E2, A("g2"), E2, OP.subtract)
+        TT(A("sf"), A("y1"), E2, OP.subtract)
+        CP(A("ls"), A("sf"))
+        Y = "yb" if t == RO - 1 else XN
+        for k in (0, 1):
+            CP(A(Y, 512 * k, 512 * k + 512), IND(A(X, 0, 2 * P), A("ls", 32 * k, 32 * k + 32)))
+            ACT(A(Y, 1024 + 512 * k, 1536 + 512 * k), IND(A(X, 0, 2 * P), A("ls", 64 + 32 * k, 96 + 32 * k)), AF.Copy)
+        if t == RO - 1:
+            for k in range(4):
+                DMA("ysys"[k], H(T.y[:, 512 * k:512 * k + 512]), A("yb", 512 * k, 512 * k + 512), "dy%d" % k)
+
+    for t in range(RO):
+        one_round(t)
+
+    n = len(ops)
+    post, left, tail = [[] for _ in ops], [len(o["pre"]) for o in ops], [0.0] * n
+    for i in range(n - 1, -1, -1):
+        o = ops[i]
+        for j in o["pre"]: post[j].append(i)
+        tail[i] = o["cost"] + o["lat"] + WAKE + max([tail[j] for j in post[i]] + [0.0])
+    pri = list(tail)
+    for i in range(n - 1, -1, -1): pri[i] = max([tail[i] + ops[i]["bon"]] + [pri[j] + ops[i]["cost"] for j in post[i]])
+    ready, free, at, order = {}, {}, [0.0] * n, []
+    for i in range(n):
+        if not left[i]: ready.setdefault(ops[i]["q"], []).append(i)
+    while len(order) < n:
+        best = None
+        for q in sorted(ready):
+            if ready[q]:
+                st = lambda i: at[i] if q == "x" else max(at[i], free.get(q, 0.0))
+                s0 = min(st(i) for i in ready[q])
+                i = max([i for i in ready[q] if st(i) <= s0 + .05], key=lambda i: (pri[i], -i))
+                if best is None or st(i) < best[0]: best = (st(i), q, i)
+        s0, q, i = best
+        ready[q].remove(i)
+        order.append(i)
+        free[q] = s0 + ops[i]["cost"]
+        for j in post[i]:
+            at[j] = max(at[j], free[q] + ops[i]["lat"] + WAKE)
+            left[j] -= 1
+            if not left[j]: ready.setdefault(ops[j]["q"], []).append(j)
+
+    clk, total, evs = {q: {} for q in list(Q) + ["x"]}, dict(arrived), {}
+    for i in order:
+        o, q, need = ops[i], ops[i]["q"], {}
+        if q == "x":
+            evs[i] = (o["ev"], {})
+            continue
+        for j in o["pre"]:
+            if evs[j] is not None:
+                (s, v), snap = evs[j]
+                if clk[q].get(s, 0) < v and need.get(s, (0,))[0] < v: need[s] = (v, snap)
+        items = sorted(need.items())
+        for s, (v, snap) in items:
+            if not any(s2 != s and sn2.get(s, 0) >= v for s2, (v2, sn2) in items): Q[q].wait_ge(T.sem[s], v)
+        for s, (v, snap) in items:
+            for s2, v2 in list(snap.items()) + [(s, v)]: clk[q][s2] = max(clk[q].get(s2, 0), v2)
+        call = o["fn"]()
+        if o["sem"] is None:
+            evs[i] = None
+            continue
+        s = o["sem"] or QS[q]
+        call.then_inc(T.sem[s], o["inc"])
+        total[s] = total.get(s, 0) + o["inc"]
+        evs[i] = ((s, total[s]), dict(clk[q]))
+    total["ls"] = sent[0]
+    for s in sorted(total):
+        g.wait_ge(T.sem[s], total[s])

@@ -3,33 +3,32 @@ from concourse.mybir import AluOpType, AxisListType, ActivationFunctionType
 
 OP, AF = AluOpType, ActivationFunctionType
 P, TW, M, RO, NR = 2048, 2048, 3, 5, 4
-NC = P // 16
-CH = [(0, 64), (64, 64)]
-SM = [0]
-SPL = [0, 1]
+NC, W = P // 16, 64
+SM = [0, 1]
+MG = [[(0, 1), (1, 3)], [(0, 3)]]
+XQV, AGV, XFV, RAV = [1, 3], [1, 3], [0, 1], [0, 2]
+GB = 64
 SELF_D = 1920
 SPX = 2 * P
-BIG = float(2 ** 24)
+BIG = float(2 ** 27)
 SENDS = {0: (1, 2, 3), 1: (1, 2, 3), 2: (1, 2), 3: (2,)}
-CY, GA, FIX, WAKE = .00083, 1.5, .03, .08
-PE, BON, LATE = [.0006], 1.0, 7.0
+CY, GA, FIX, WAKE = .001, 1.3, .02, .1
+PE, BON, LATE, PASSES = [.0005], 1.0, 7.0, 8
 
 SCRATCH = {}
 for _d, _l in {
-    "float32": "idnf 128 nf 128 xf 2048 cf 32 kmf 16 grp 128 m16 16 emn 128 nt 128 nt8 128 ntm 128 pt 128 v3 128 vmn 128 b4 128 bq 128 "
-               "lo 128 key 128 lod 128 prd 128 prh 128 prk 128 k2a 128 k2 128 rn 128 bs 128 y1 128 g2 128 sf 128 nb2 128 dg 16 dg2 16 "
-               "c 64 nc 16 upd 64 land 192",
-    "bfloat16": "xa 4112 xb 4112 tmo 2048 tb1 2064 tb2 2064 tb3 2064 xq 2048 ag 2048 az 2048 yb 2048 bm 2048 wb 2048 mf 2048 mz 2048 "
-                "xs 2048 as 2048 idm 128 ma 128 mb 128 idn 128 idf 128 idj 128 idk 128 ids 128 idc 128 id1 128 id2 128 em 128 one 64 "
-                "eqb 384 sg 128 nd 16",
-    "float16": "mn 6144 md 2048 q16 384 id16 128",
-    "int32": "io2 2048 ic 128 ipart 4 ci 16 wti 4 kmi 16 tmpi 128 tmpj 128 ui 128 u 128 sq 128 s5 128 t3 384 q3 384 vm 128 qs 128 b1 128 "
-             "ri 128 uq 128 hp 128 hs 128 ki 128 kv 128 cii 16",
+    "float32": "idnf 128 xf 2048 cf 40 kmf 16 kmt 16 grp 128 m16 16 nt 128 v3 128 vmn 128 ku 384 nf 128 uv 128 uf 128 key 128 prd 128 prh 128 prk 128 "
+               "rn 128 gm 128 dg 16 dg2 32 def 8 c 64 nc 16 upd 64 land 192",
+    "bfloat16": "xa 4112 xb 4112 tmo 2048 tb1 2064 tb2 2064 tb3 2064 xq 2048 ag 2048 az 2048 yb 2048 wb 144 mf 144 mz 144 ml 144 "
+                "xs 2048 as 2048 ic 144 ig 128 emn 128 idm 128 ma 128 mb 128 idn 128 idf 128 idj 128 idk 128 ids 128 id1 128 "
+                "id2 128 idu 128 idb 128 idh 128 idi 128 em 128 one 128 eqb 384 ido 128 nd 16 ru 128 rq 128 e0 128 e2 128 ib 128 nm 16",
+    "float16": "mn 6144 md 144 q16 384 id16 128 id8 128 idm16 128 grp16 128 nt16 128 na 128 nb 128 lod 128 ta 128 tb 128 tc 128 s 16",
+    "int32": "ipart 4 ci 16 wti 4 kmi 16 t3 384 q3 384 vm 128 qs 128 b1 128 hp 128 hs 128 cii 16",
     "uint16": "l3 384 lq 128 lh 128 ls 128 l1 16"}.items():
     _w = _l.split()
     for _i in range(0, len(_w), 2):
         SCRATCH[_w[_i]] = ("sbuf", [128, int(_w[_i + 1])], _d)
-PSUMS = ["ps0", "ps1", "ps2", "ps3", "ps5", "z0", "z1", "z2"]
+PSUMS = ["ps0", "pu", "pq", "pk1", "pk2", "z0", "z1", "z2"]
 for _n in PSUMS:
     SCRATCH[_n] = ("psum", [128, 512], "float32")
 SEMAPHORES = ["qv", "qs", "qp", "qg", "dx0", "dx1", "dw", "dk", "dt", "dy0", "dy1", "dy2", "dy3", "ls", "tma1", "tma2", "tma3"] + \
@@ -57,12 +56,14 @@ def rank_program(g, core, T, topo):
         for (n, a, b), k in R:
             for d, w2 in ((wr, 1), (rd, 0)):
                 for a2, b2, q2, i2 in d.setdefault(n, []):
-                    if (n in PSUMS and q2 != q) or (a < b2 and a2 < b and (k or w2)):
+                    if (n in PSUMS and (q2 != q or q == "p")) or (a < b2 and a2 < b and (k or w2)):
                         pre.add(i2)
         for (n, a, b), k in R:
             if k and n not in PSUMS:
                 for d in (wr, rd):
                     d[n] = [x for x in d[n] if not (a <= x[0] and x[1] <= b)]
+            if n in PSUMS and q == "p":
+                wr[n], rd[n] = [], []
             (wr if k else rd)[n].append((a, b, q, me))
         pre.discard(me)
         ops.append(dict(q=q, fn=fn, pre=sorted(pre), cost=cost, bon=bon[0], sem=sem, inc=inc, lat=lat, ev=ev))
@@ -71,7 +72,7 @@ def rank_program(g, core, T, topo):
     def vcost(o, ins, two=False, half=False):
         n = max([x[2] for x in ins] + [o[2]])
         for x in ins + [o]:
-            if x[2] < 0: return -x[2] * CY * (GA if x is not o else 3) + FIX + .05
+            if x[2] < 0: return -x[2] * CY * (GA if x is not o else 3) + .05
         ps = any(x[1][0][0] in PSUMS for x in ins)
         if two and not ps: n *= 2
         if half and not ps and all(SCRATCH.get(x[1][0][0], ("", "", ""))[2] in ("bfloat16", "float16", "uint16") for x in ins + [o]): n //= 2
@@ -105,6 +106,10 @@ def rank_program(g, core, T, topo):
         note("s", lambda: g.scalar.activation(o[0], x[0], func, **kw), [o],
              [x] + [s for s in (bias, scale) if isinstance(s, tuple)], vcost(o, [x]) + .015)
 
+    def COPY(o, x, vec):
+        if vec: CP(o, x)
+        else: ACT(o, x, AF.Copy)
+
     def MM(o, pairs, start=True, stop=True):
         def go():
             for i, z in enumerate(pairs):
@@ -117,80 +122,74 @@ def rank_program(g, core, T, topo):
         note(q, lambda: Q[q].dma_start(o[0], x[0]), [o], [x], .1, sem, 16, 4.0)
 
     def SUMS(mat, buf, base, n):
-        return [(A(mat, jj * 128, jj * 128 + 128), A(buf, base + jj, base + 16 * n, 16)) for jj in range(16)]
+        return [(A(mat, 15 - jj, 143 - jj), A(buf, base + jj, base + 16 * n, 16)) for jj in range(16)]
 
-    def IOTA(pattern, b, cm, base=0):
-        note("g", lambda: g.iota(b[0], pattern, base, cm), [b], [], .13 + 2 * b[2] * CY)
+    def IOTA(pattern, b, cm, small=True):
+        kw = {"allow_small_or_imprecise_dtypes": True} if small else {}
+        note("g", lambda: g.iota(b[0], pattern, 0, cm, **kw), [b], [], .13 + 2 * b[2] * CY)
 
     def H(ap):
         return (ap, [], 0)
 
+    DMA("s", A("tmo"), H(T.tm[:]), "dt")
     DMA("y", A("wti", 0, 1), H(T.wt[:]), "dw")
     DMA("y", A("xa", 0, P // 2), H(T.x[:, 0:P // 2]), "dx0")
-    DMA("s", A("tmo"), H(T.tm[:]), "dt")
     DMA("y", A("xa", P // 2, P), H(T.x[:, P // 2:P]), "dx1")
     DMA("y", A("kmi", 0, 15), H(T.km[:]), "dk")
 
-    IOTA([[0, 1]], A("ipart", 0, 1), 1)
-    IOTA([[1, 128]], A("ic"), 0)
-    for k in (0, 1):
-        IOTA([[-1000, 8], [1, 8], [1000, 16]], A("io2", 1024 * k, 1024 * k + 1024), 0, -8000 * k)
+    IOTA([[0, 1]], A("ipart", 0, 1), 1, False)
+    IOTA([[1, 144]], A("ic"), 0)
+    IOTA([[1, 8], [0, 16]], A("ig"), 0)
     C = lambda i: A("cf", i, i + 1)
-    (JJ, GK, IPF, F15, R15N, FIRST, NF, ODD, MH, SX, ST, CW, CMD, CMF, CMZ, CJ, CK, CB, CTH, CC2, C2047, C8K, CMH2, CQ, CP23, CM23, C1,
-     CM2047) = [C(i) for i in range(28)]
+    (JJ, GK, IPF, F15, R15, FIRST, NF, ODD, MH, SX, ST, CW, CMD, CMF, CMZ, CML, CJ, CK, G15, CMH2, CMFN,
+     CR, CQ, CM129, C1, CM1, CM2, CMH, C2049, C2047, CB5) = [C(i) for i in range(31)]
     TS(A("ci", 0, 1), A("ipart", 0, 1), 15, OP.bitwise_and)
     TS(A("ci", 1, 2), A("ipart", 0, 1), 4, OP.arith_shift_right)
     TS(A("ci", 2, 3), A("ipart", 0, 1), 1, OP.bitwise_and)
     CP(JJ, A("ci", 0, 1)); CP(GK, A("ci", 1, 2)); CP(ODD, A("ci", 2, 3)); CP(IPF, A("ipart", 0, 1))
-    TS(F15, JJ, 15.0, OP.is_lt)
-    TS(FIRST, JJ, 0.0, OP.is_equal)
-    TS(NF, JJ, 0.0, OP.is_gt)
-    CP(CW, A("wti", 0, 1))
+    for b, v in ((CR, 2.0 ** -13 - .5), (CQ, 128.75), (CM129, -129.0), (C1, 1.0), (CM1, -1.0), (CM2, -8192.0 * SELF_D), (CMH, -.5), (C2049, 2049.0),
+                 (CB5, -4096.5), (A("one"), 1.0), (A("nd"), 0.0), (A("upd"), 0.0), (A("def", 0, 1), 2047.0), (A("dg2", 16, 17), 1.5 * 2 ** 22)):
+        FILL(b, v)
+    TS(G15, A("ci", 1, 2), 16.0, OP.mult, 15.0, OP.add)
+    TS(F15, A("ci", 0, 1), 15.0, OP.is_lt)
+    TS(R15, A("ci", 0, 1), 15.0, OP.is_equal)
+    TS(FIRST, A("ci", 0, 1), 0.0, OP.is_equal)
+    TS(NF, A("ci", 0, 1), 0.0, OP.is_gt)
+    TS(CW, A("wti", 0, 1), 2.0 ** -12, OP.mult)
     TS(CMD, F15, -8192.0, OP.mult, -8192.0, OP.add)
-    TS(CMF, F15, 8192.0, OP.mult)
-    TS(CMZ, F15, 2047.0, OP.mult, 1.0, OP.add)
+    TS(CMZ, F15, 8188.0, OP.mult, 4.0, OP.add)
     TS(CJ, F15, 2.0, OP.mult, -1.0, OP.add)
-    TS(CK, F15, -2.0, OP.mult)
-    TS(R15N, F15, 1.0, OP.mult, -1.0, OP.add)
-    TS(CB, R15N, -1.0, OP.mult)
-    TS(MH, F15, 0.5, OP.mult)
-    TS(CMH2, MH, -1.0, OP.mult, 1.0, OP.add)
+    ACT(CMF, F15, AF.Copy, None, 8192.0)
+    ACT(CML, R15, AF.Copy, None, -4096.0)
+    ACT(CK, F15, AF.Copy, None, -2.0)
+    ACT(MH, F15, AF.Copy, None, .5)
+    ACT(CMH2, MH, AF.Identity, C1, -1.0)
     TS(SX, JJ, float(SPX), OP.add, NF, OP.mult)
     TS(ST, JJ, float(TW), OP.add, NF, OP.mult)
-    for b, v in ((CTH, -8192.0 * (SELF_D - 7)), (CC2, 1024.0 * SELF_D), (C2047, 2047.0), (C8K, 8192.0), (CQ, -0.25),
-                 (CP23, 8388608.0), (CM23, -8388608.0), (C1, 1.0), (CM2047, -2047.0)):
-        FILL(b, v)
-    TS(A("idn"), A("ic"), IPF, OP.is_equal)
-    TS(A("tmpi"), A("ic"), 4, OP.arith_shift_right)
-    TS(A("grp"), A("tmpi"), GK, OP.is_equal)
-    TS(A("tmpj"), A("ic"), 15, OP.bitwise_and)
-    TS(A("emn"), A("tmpj"), 15.0, OP.is_equal, F15, OP.mult)
-    TT(A("prd"), A("emn"), A("grp"), OP.mult)
-    TS(A("idf"), A("idn"), F15, OP.mult)
-    TT(A("em"), A("idf"), A("prd"), OP.subtract)
-    for k in (0, 1):
-        TS(A("wb", 1024 * k, 1024 * k + 1024), A("io2", 1024 * k, 1024 * k + 1024), GK, OP.is_equal, CW, OP.mult)
-    TS(A("md"), A("io2"), GK, OP.is_equal, CMD, OP.mult)
-    TS(A("bm"), A("io2"), GK, OP.is_equal)
-    ACT(A("mf"), A("bm"), AF.Copy, None, CMF)
-    ACT(A("mz"), A("bm"), AF.Copy, None, CMZ)
-    CP(A("kmf", 0, 15), A("kmi", 0, 15))
-    TS(A("nt"), A("ic"), 16.0, OP.mult, JJ, OP.add)
-    TS(A("nt8"), A("nt"), 8.0, OP.mult, -8192.0, OP.add)
-    TS(A("ntm"), A("nt"), -2047.0, OP.add)
-    PL = A("ps0", 0, 128)
-    CP(PL, A("nt"))
-    TS(A("idj"), A("idn"), CJ, OP.mult)
-    TS(A("idk"), A("idn"), CK, OP.mult)
-    TS(A("ids"), A("idn"), float(SELF_D * 8192), OP.mult)
-    TS(A("idc"), A("idn"), float(SELF_D * 1024), OP.mult)
-    TS(A("id1"), A("idn"), 2048.0, OP.mult)
-    TS(A("id2"), A("idn"), 4096.0, OP.mult)
-    TS(A("idm"), A("idn"), -1.0, OP.mult)
-    TS(A("id16"), A("ic"), IPF, OP.is_equal)
-    TS(A("idnf"), A("ic"), IPF, OP.is_equal)
+    for m, cw in (("wb", CW), ("md", CMD), ("mf", CMF), ("mz", CMZ), ("ml", CML)):
+        TS(A(m), A("ic"), G15, OP.is_equal, cw, OP.mult)
+    IC = A("ic", 0, 128)
+    TS(A("idn"), IC, IPF, OP.is_equal)
+    TS(A("grp"), A("ig"), GK, OP.is_equal)
+    TS(A("grp16"), A("ig"), GK, OP.is_equal)
+    TS(A("emn"), IC, G15, OP.is_equal, F15, OP.mult)
+    TS(A("idf"), IC, IPF, OP.is_equal, F15, OP.mult)
+    TT(A("em"), A("idf"), A("emn"), OP.subtract)
+    TS(A("kmt", 0, 15), A("kmi", 0, 15), 1024.0, OP.is_ge, -2048.0, OP.mult)
+    TT(A("kmt", 0, 15), A("kmt", 0, 15), A("kmi", 0, 15), OP.add)
+    TS(A("kmf", 0, 15), A("kmt", 0, 15), -32768.0, OP.mult)
+    TS(A("kmt", 0, 15), A("kmf", 0, 15), .5, OP.mult)
+    TS(A("nt"), IC, 16.0, OP.mult, JJ, OP.add)
+    TS(A("nt16"), IC, 16.0, OP.mult, JJ, OP.add)
+    for m, v in (("id16", 1.0), ("id8", 8.0), ("idm16", -1.0)):
+        TS(A(m), IC, IPF, OP.is_equal, v, OP.mult)
+    for m, v in (("idu", 129.0), ("idm", -1.0), ("ids", SELF_D * 16384.0), ("ido", SELF_D * -8192.0), ("id1", 2048.0), ("id2", 4096.0), ("idj", CJ),
+                 ("idk", CK), ("idnf", 1.0), ("idb", BIG), ("idh", .5), ("idi", -.5)):
+        ACT(A(m), A("idn"), AF.Copy, None, v)
     TS(A("m16"), A("ic", 0, 16), JJ, OP.is_equal)
-    FILL(A("one"), 1.0); FILL(A("nd"), 0.0); FILL(A("upd"), 0.0)
+    for i in (0, 1):
+        for m in range(M):
+            MM(A("ps0", 192 * i + W * m, 192 * i + W * m + W), [(A("id16"), A("nt16", W * i, W * i + W))])
 
     sent, arrived = [0], {}
 
@@ -206,6 +205,7 @@ def rank_program(g, core, T, topo):
 
     cc = lambda i: A("c", i, i + 1)
     ii = lambda i: A("cii", i, i + 1)
+    ss = lambda i: A("s", i, i + 1)
     seen, landed = set(), {}
 
     def updates(t):
@@ -247,231 +247,235 @@ def rank_program(g, core, T, topo):
     def one_round(t):
         X, XN = ("xa", "xb") if t % 2 == 0 else ("xb", "xa")
         TB = "tb%d" % (1 + t % 3)
-        MM(A("ps1", 0, 128), SUMS("wb", X, 0, NC))
-        for k in range(4):
-            b = A(["z2", "z0", "z1", "ps2"][k])
-            MM(b, [(A("em"), A(X, 512 * k, 512 * k + 512))])
-            ACT(A("xf", 512 * k, 512 * k + 512), b, AF.Identity, R15N)
-        for k in range(4):
-            ACT(A(X, P + 512 * k, P + 512 * k + 512), A(X, 512 * k, 512 * k + 512), AF.Identity, CB, CJ)
-        MM(A("ps5", 0, 128), SUMS("mf", X, 0, NC))
-        CP(A("ui"), A("ps1", 0, 128))
-        TS(A("u"), A("ui"), 4095, OP.bitwise_and)
-        TT(A("sq"), A("u"), A("u"), OP.mult)
-        TS(A("s5"), A("sq"), 5, OP.arith_shift_right)
-        for m in range(M):
-            a, b = 128 * m, 128 * m + 128
-            TS(A("ps0", a + 128, b + 128), A("u"), A("kmf", 3 * t + m, 3 * t + m + 1), OP.mult)
-            TT(A("t3", a, b), A("s5"), A("ps0", a + 128, b + 128), OP.add)
-            TS(A("q3", a, b), A("t3", a, b), P - 1, OP.bitwise_and)
-            CP(A("l3", a, b), A("q3", a, b))
-            TT(A("eqb", a, b), A("q3", a, b), PL, OP.is_equal)
-            CP(A("q16", a, b), A("q3", a, b))
-        ACT(A("nf"), A("ps5", 0, 128), AF.Identity, C8K, -1.0)
-        TT(A("pt"), A("nt8"), A("ps5", 0, 128), OP.add)
+        ONE = A("one", 0, W)
+        ch = lambda n, i, off=0: A(n, off + W * i, off + W * i + W)
+        c3 = lambda n, i, m0, m1: A(n, 192 * i + W * m0, 192 * i + W * m1)
 
-        def pick(out, tab, lst, a, b, i):
-            for k, h in enumerate(range(a, b, 32)):
-                o, x = A(out, 16 * h, 16 * min(h + 32, b)), IND(A(tab, 0, P), A(lst, h, min(h + 32, b)))
-                if i in SPL and k % 2: CP(o, x)
-                else: ACT(o, x, AF.Copy)
+        def weighted(out, o, buf, i, r):
+            MM(o, SUMS("wb", buf, 16 * W * i, W) + [(A("idu"), ONE)])
+            ACT(r, o, AF.Identity, CR)
+            TT(out, r, o, OP.subtract)
 
-        def near(c, i):
-            c0, n = c
-            a = 16 * c0
-            e = lambda m: A("eqb", 128 * m + c0, 128 * m + c0 + n)
-            k = lambda m: A("q16", 128 * m + c0, 128 * m + c0 + n)
-            l = lambda m: A("l3", 128 * m + c0, 128 * m + c0 + n)
-            o0, o1 = A("ps2", 0, n), A("ps2", n, 2 * n)
+        def lists(i):
+            u, sq = ch("uv", i), ch("pq", i)
+            weighted(u, A("pu" if i == 0 else "pk2", 0, W), X, i, ch("ru", i))
+            ACT(sq, u, AF.Square, None, 2048.0)
+            for m in range(M):
+                ACT(c3("ku", i, m, m + 1), u, AF.Identity, A("kmt", 3 * t + m, 3 * t + m + 1), A("kmf", 3 * t + m, 3 * t + m + 1))
+            ACT(ch("uf", i), u, AF.Copy, None, 2.0 ** 24)
+            for m0, m1 in MG[i]:
+                for m in range(m0, m1):
+                    TT(c3("t3", i, m, m + 1), c3("ku", i, m, m + 1), sq, OP.add)
+                TS(c3("q3", i, m0, m1), c3("t3", i, m0, m1), 3, OP.arith_shift_right, P - 1, OP.bitwise_and)
+                CP(c3("l3", i, m0, m1), c3("q3", i, m0, m1))
+            TT(c3("eqb", i, 0, M), c3("q3", i, 0, M), c3("ps0", i, 0, M), OP.is_equal)
+            CP(c3("q16", i, 0, M), c3("l3", i, 0, M))
+
+        def pick(out, tab, lst, i, vec):
+            for k in (2 * i, 2 * i + 1):
+                COPY(A(out, 512 * k, 512 * k + 512), IND(A(tab, 0, P), A(lst, 32 * k, 32 * k + 32)), k in vec)
+
+        def near(i):
+            a, n = 16 * W * i, W
+            o0, o1, o2 = A("pk1", 0, n), A("pk1", n, 2 * n), A("pk2", 0, n)
             for m in range(2 if i in SM else 3):
-                TT(A("mn", 3 * a + 16 * n * m, 3 * a + 16 * n * (m + 1)), IND(A("xf"), l(m)), A(X, a, a + 16 * n), OP.min)
-            MM(A("ps2", 0, 2 * n), SUMS("md", "mn", 48 * c0, 2 * n) +
-               [(A("ids"), e(0), o0), (A("ids"), e(1), o1), (A("id1"), A("one", 0, n), o1), (A("id16"), k(0), o0), (A("id16"), k(1), o1)])
-            last = [(A("ids"), e(2)), (A("id2"), A("one", 0, n)), (A("id16"), k(2))]
+                for h in range(0, n, GB):
+                    TT(A("mn", 3 * a + 16 * (n * m + h), 3 * a + 16 * (n * m + h + GB)),
+                       IND(A("xf"), A("l3", 192 * i + n * m + h, 192 * i + n * m + h + GB)), A(X, a + 16 * h, a + 16 * (h + GB)), OP.min)
+            low = lambda m: [(A("ids"), c3("eqb", i, m, m + 1)), (A("id16"), c3("q16", i, m, m + 1))] + ([(A("id%d" % m), ONE)] if m else [])
+            mins = lambda m: SUMS("md", "mn", 3 * a + 16 * n * m, n) + [(A("idnf"), ch("nf", i))] + low(m)
+            MM(o0, mins(0))
+            ACT(ch("v3", i), o0, AF.Copy)
+            MM(o1, mins(1))
             if i in SM:
-                for p0 in range(a, a + 16 * n, 512):
-                    p1 = min(p0 + 512, a + 16 * n)
-                    w = A("z2", 0, p1 - p0)
-                    ACT(A("xs", p0, p1), IND(A(X, 0, P), A("l3", 256 + p0 // 16, 256 + p1 // 16)), AF.Copy)
-                    MM(w, [(A("idm"), A(X, p0, p1)), (A("idn"), A("xs", p0, p1))])
-                    ACT(A("as", p0, p1), w, AF.Abs)
-                MM(A("ps3", 0, n), SUMS("mf", "as", a, n) + last + [(A("idnf"), A("nf", c0, c0 + n))])
+                for k, p0 in enumerate(range(a, a + 16 * n, 512)):
+                    w, l0 = A("z%d" % (2 - k)), 192 * i + 2 * n + 32 * k
+                    ACT(A("xs", p0, p0 + 512), IND(A(X, 0, P), A("l3", l0, l0 + 32)), AF.Copy)
+                    MM(w, [(A("idm"), A(X, p0, p0 + 512)), (A("idn"), A("xs", p0, p0 + 512))])
+                    ACT(A("as", p0, p0 + 512), w, AF.Abs)
+                MM(o2, SUMS("mf", "as", a, n) + [(A("ido"), ONE)] + low(2))
             else:
-                MM(A("ps3", 0, n), SUMS("md", "mn", 48 * c0 + 32 * n, n) + last)
-            ACT(A("v3", c0, c0 + n), o0, AF.Copy)
-            TT(A("vmn", c0, c0 + n), A("v3", c0, c0 + n), o1, OP.min)
+                MM(o2, mins(2))
+            TT(ch("vmn", i), ch("v3", i), o1, OP.min)
+            TT(ch("vm", i), ch("vmn", i), o2, OP.min)
+            TS(ch("qs", i), ch("vm", i), P - 1, OP.bitwise_and)
+            CP(ch("lq", i), ch("qs", i))
+            TS(ch("b1", i), ch("vm", i), -8192, OP.bitwise_and)
 
-        def choose(c, i):
-            a, b, n = c[0], c[0] + c[1], c[1]
-            TT(A("vm", a, b), A("vmn", a, b), A("ps3", 0, n), OP.min)
-            TS(A("qs", a, b), A("vm", a, b), P - 1, OP.bitwise_and)
-            CP(A("lq", a, b), A("qs", a, b))
-            pick("xq", X, "lq", a, b, i)
-            MM(A("ps5", 128, 128 + n), SUMS("wb", "xq", 16 * a, n))
-            TS(A("b1", a, b), A("vm", a, b), -8192, OP.bitwise_and)
-            TT(A("b4", a, b), A("b1", a, b), A("pt", a, b), OP.add)
-            ACT(A("sg", a, b), A("b4", a, b), AF.Sign, CTH)
-            ACT(A("bq", a, b), A("b4", a, b), AF.Identity, CC2, 0.25)
-            TT(A("lo", a, b), A("qs", a, b), A("ps0", a, b), OP.min)
-
-        def asked(c, i):
-            a, b, n = c[0], c[0] + c[1], c[1]
-            CP(A("ri", a, b), A("ps5", 128, 128 + n))
-            TS(A("uq", a, b), A("ri", a, b), 4095, OP.bitwise_and)
-            TT(A("hp", a, b), A("uq", a, b), A("u", a, b), OP.mult)
-            TS(A("hs", a, b), A("hp", a, b), 4, OP.arith_shift_right, TW - 1, OP.bitwise_and)
-            CP(A("lh", a, b), A("hs", a, b))
-            sg = [(A("z%d" % (k % 2), 0, min(512, 16 * b - p0)), p0, min(p0 + 512, 16 * b)) for k, p0 in enumerate(range(16 * a, 16 * b, 512))]
+        def asked(i):
+            pick("xq", X, "lq", i, XQV)
+            uq = ch("ps0", i, 384)
+            weighted(uq, A("pu", 0, W), "xq", i, ch("rq", i))
+            TT(ch("hp", i), ch("uf", i), uq, OP.mult)
+            TS(ch("hs", i), ch("hp", i), 4, OP.arith_shift_right, TW - 1, OP.bitwise_and)
+            CP(ch("lh", i), ch("hs", i))
+            sg = [(A("z%d" % (k % 3)), 512 * k, 512 * k + 512) for k in (2 * i, 2 * i + 1)]
             for z, p0, p1 in sg:
-                MM(z, [(A("idj"), A(X, p0, p1)), (A("idn"), A("xq", p0, p1))], True, False)
-            pick("ag", TB, "lh", a, b, i)
+                MM(z, [(A("idj"), A(X, p0, p1))], True, False)
+                MM(z, [(A("idn"), A("xq", p0, p1))], False, False)
+            pick("ag", TB, "lh", i, AGV)
             for z, p0, p1 in sg:
                 MM(z, [(A("idk"), A("ag", p0, p1))], False, True)
                 ACT(A("az", p0, p1), z, AF.Abs)
 
-        def keyed(c):
-            a, b = c[0], c[0] + c[1]
-            MM(A("ps1", a, b), SUMS("mz", "az", 16 * a, c[1]) + [(A("idc"), A("sg", a, b))])
-            TT(A("key", a, b), A("bq", a, b), A("ps1", a, b), OP.add)
+        def keyed(i):
+            o, l = ch("pq", i, 256), ch("pk1", i, 128)
+            MM(o, SUMS("mz", "az", 16 * W * i, W) + [(A("id8"), ch("nt16", i))])
+            TT(ch("key", i), ch("b1", i), o, OP.add)
+            MM(l, SUMS("ml", "az", 16 * W * i, W) + [(A("id16"), ch("nt16", i))])
+            TT(ch("lod", i), ch("qs", i), l, OP.min)
 
-        AC, BC, INV, NIN, BA, B1, B1I, RD, SL, BS, AB, RI = [cc(i) for i in range(10, 22)]
-        E0, E1, E2 = [A("ps0", 128 * m + 128, 128 * m + 256) for m in range(3)]
+        for i in (0, 1):
+            bon[0] = BON * (2 - i)
+            lists(i)
+        bon[0] = BON * 2
+        for k in range(4):
+            b = A(["z0", "z1", "z2", "pk1"][k])
+            MM(b, [(A("em"), A(X, 512 * k, 512 * k + 512))])
+            COPY(A("xf", 512 * k, 512 * k + 512), b, k in XFV)
+        bon[0] = 0.0
+        for k in range(4):
+            ACT(A(X, P + 512 * k, P + 512 * k + 512), A(X, 512 * k, 512 * k + 512), AF.Identity, R15, CJ)
+        bon[0] = BON * 2
+        MM(A("pu", 128, 256), SUMS("mf", X, 0, NC))
+        ACT(A("nf"), A("pu", 128, 256), AF.Identity, CM2)
         updates(t)
-        for i, c in enumerate(CH):
-            bon[0] = BON * (len(CH) - i)
-            near(c, i)
-            choose(c, i)
-            asked(c, i)
-        for i, c in enumerate(CH):
-            bon[0] = BON * (len(CH) - i)
-            keyed(c)
-            a, b = c[0], c[0] + c[1]
-            e = A("ps0", 128 + a, 128 + b)
-            CP(A("ki", a, b), A("key", a, b))
-            TS(A("kv", a, b), A("ki", a, b), 1, OP.bitwise_and)
-            TS(e, A("kv", a, b), -4096.0, OP.mult)
-            TT(A("lod", a, b), A("lo", a, b), e, OP.add)
+        for i in (0, 1):
+            bon[0] = BON * (2 - i)
+            near(i)
+        for i in (0, 1):
+            bon[0] = BON * (2 - i)
+            asked(i)
+        for i in (0, 1):
+            bon[0] = BON * (2 - i)
+            keyed(i)
         bon[0] = 0.0
 
-        def lowest(src, out, dg):
-            RED(out, src, OP.min)
-            TS(A(dg), A("m16"), out, OP.mult)
-            MM(A("ps1", 0, 16), [(A("grp"), A(dg))])
-
-        lowest(A("key"), cc(0), "dg")
-        RED(cc(1), A("ps1", 0, 16), OP.min)
-        TS(E1, A("key"), cc(1), OP.is_equal)
-        TT(A("prd"), A("qs"), E1, OP.mult)
-        RED(cc(2), A("prd"), OP.add)
-        MM(A("ps1", 0, 1), [(A("grp"), cc(2))])
+        K0, K1, Q0, H0, K2, K3, Q2, MK, HI, LO, MV, AC, BC, INV, NIN, NN, N2, NB, SL, BA, RD, BS, TA = [cc(i) for i in range(23)]
+        E, B1I = A("ps0", 384, 512), A("def", 1, 2)
+        KEY, KM = A("key"), A("z1", 0, NC)
+        RED(K0, KEY, OP.min)
+        TS(A("dg"), A("m16"), K0, OP.mult)
+        MM(A("pu", 0, 16), [(A("grp"), A("dg"))])
+        TS(E, KEY, K0, OP.is_equal)
+        TT(A("prd"), A("qs"), E, OP.mult)
+        RED(K1, A("pu", 0, 16), OP.min)
+        RED(Q0, A("prd"), OP.add)
+        TS(ss(0), K0, K1, OP.is_equal, Q0, OP.mult)
+        MM(A("pu", 16, 17), [(A("grp16"), ss(0))])
+        MM(KM, [(A("idnf"), KEY)], True, False)
+        CP(ii(0), K1)
+        TS(ii(1), ii(0), 3, OP.arith_shift_right, P - 1, OP.bitwise_and)
+        TS(ii(2), ii(0), 4, OP.bitwise_and)
+        TS(INV, ii(2), .25, OP.mult)
+        TT(AC, ii(1), A("pu", 16, 17), OP.min)
+        TT(BC, ii(1), A("pu", 16, 17), OP.max)
         if t < RO - 1:
-            TT(A("prh"), A("hs"), E1, OP.mult)
-            RED(cc(27), A("prh"), OP.add)
-            MM(A("ps3", 64, 65), [(A("grp"), cc(27))])
-            CP(A("upd", 16 * t + 1, 16 * t + 2), A("ps3", 64, 65))
-        CP(ii(0), cc(1))
-        TS(ii(1), ii(0), 1, OP.arith_shift_right, P - 1, OP.bitwise_and)
-        TS(ii(2), ii(0), 1, OP.bitwise_and)
-        CP(INV, ii(2))
+            TT(A("prh"), A("hs"), E, OP.mult)
+            RED(H0, A("prh"), OP.add)
+            TS(ss(2), K0, K1, OP.is_equal, H0, OP.mult)
+            MM(A("pq", 0, 1), [(A("grp16"), ss(2))])
+            ACT(A("upd", 16 * t + 1, 16 * t + 2), A("pq", 0, 1), AF.Copy)
+        ACT(A("ib"), A("one"), AF.Copy, None, INV)
+        TS(A("e0"), A("lod"), AC, OP.is_le)
+        TS(A("e2"), A("lod"), BC, OP.is_ge)
+        MM(KM, [(A("idb"), A("ib")), (A("idb"), A("e0")), (A("idb"), A("e2"))], False, True)
+        RED(K2, KM, OP.min)
+        TS(A("dg2", 0, 16), A("m16"), K2, OP.mult)
+        MM(A("pu", 0, 17), [(A("grp"), A("dg2", 0, 17))])
+        TS(E, KM, K2, OP.is_equal)
+        TT(A("prk"), A("qs"), E, OP.mult)
+        RED(K3, A("pu", 0, 17), OP.min)
+        RED(Q2, A("prk"), OP.add)
+        CP(ii(4), K2)
+        TS(ii(5), ii(4), 3, OP.arith_shift_right, P - 1, OP.bitwise_and)
         ACT(NIN, INV, AF.Identity, C1, -1.0)
-        TT(AC, ii(1), A("ps1", 0, 1), OP.min)
-        TT(BC, ii(1), A("ps1", 0, 1), OP.max)
-        TS(E0, A("lod"), AC, OP.is_le, BIG, OP.mult)
-        TT(A("k2a"), A("key"), E0, OP.max)
-        TS(E2, A("lod"), BC, OP.is_ge, BIG, OP.mult)
-        TT(A("k2"), A("k2a"), E2, OP.max)
-        lowest(A("k2"), cc(3), "dg2")
-        RED(cc(4), A("ps1", 0, 16), OP.min)
-        TS(E0, A("k2"), cc(4), OP.is_equal)
-        TT(A("prk"), A("qs"), E0, OP.mult)
-        RED(cc(5), A("prk"), OP.add)
-        MM(A("ps1", 0, 1), [(A("grp"), cc(5))])
-        CP(ii(4), cc(4))
-        TS(ii(5), ii(4), 1, OP.arith_shift_right, P - 1, OP.bitwise_and)
-        TS(cc(6), cc(4), BIG, OP.is_lt, NIN, OP.mult)
-        ACT(BA, AC, AF.Identity, BC, -1.0)
-        ACT(RD, BA, AF.Copy, None, NIN)
-        ACT(RI, INV, AF.Identity, RD, float(P + 1))
-        ACT(AB, AC, AF.Identity, BC)
-        ACT(BS, AB, AF.Identity, RI, INV)
+        ACT(NN, INV, AF.Identity, CM1)
+        ACT(N2, NIN, AF.Copy, None, 2047.0)
+        ACT(NB, INV, AF.Identity, CB5, 4096.0)
         ACT(SL, INV, AF.Copy, None, -2.0)
-        ACT(A("rn"), A("nt"), AF.Identity, BS, SL)
-        ACT(A("nb2"), A("ntm"), AF.Identity, BA)
-        ACT(B1, BC, AF.Identity, C2047, -1.0)
-        ACT(B1I, B1, AF.Copy, None, NIN)
-        ACT(cc(32), BC, AF.Identity, CM2047)
-        TS(A("l1", 0, 1), ODD, BA, OP.mult, AC, OP.add)
-        ACT(A("nc"), IND(A(X, 0, P), A("l1", 0, 1)), AF.Copy)
-        TS(A("l1", 2, 3), FIRST, AC, OP.mult, SX, OP.add)
-        ACT(cc(22), A("nc", 0, 1), AF.Identity, CQ, CMH2)
-        ACT(cc(28), A("nc", 1, 2), AF.Identity, cc(22), MH)
-        ACT(cc(29), cc(28), AF.Identity, CP23)
-        ACT(A("nd", 0, 1), cc(29), AF.Identity, CM23)
-        CP(IND(A(X), A("l1", 2, 3)), A("nd"))
-        if t < RO - 1:
-            ACT(A("upd", 16 * t, 16 * t + 1), A("nd", 0, 1), AF.Copy)
-            send_new(t)
-        ACT(cc(30), AC, AF.Copy, None, -1.0)
-        ACT(cc(31), BC, AF.Copy, None, -1.0)
+        ACT(B1I, BC, AF.Identity, N2, NN)
+        ACT(BA, AC, AF.Identity, BC, -1.0)
+        ACT(cc(30), AC, AF.Identity, CMH, -1.0)
+        ACT(cc(31), BC, AF.Identity, NB, -1.0)
         ACT(A("ma"), A("nt"), AF.Sign, cc(30))
         ACT(A("mb"), A("nt"), AF.Sign, cc(31))
-        ACT(A("ma"), A("ma"), AF.Relu)
-        ACT(A("mb"), A("mb"), AF.Relu, None, INV)
-        MM(A("z0", 0, 128), [(A("idn"), A("ma")), (A("idm"), A("mb"))])
-        TT(E2, A("rn"), A("z0", 0, 128), OP.mult)
-        TT(A("bs"), A("nt"), E2, OP.add)
-        TT(cc(8), ii(5), A("ps1", 0, 1), OP.max)
-        TT(cc(7), ii(5), A("ps1", 0, 1), OP.min)
-        TS(cc(9), cc(8), BC, OP.is_gt, cc(6), OP.mult)
-        TT(cc(23), cc(8), cc(7), OP.subtract)
-        TS(cc(25), cc(23), cc(32), OP.add, cc(9), OP.mult)
-        TS(cc(24), cc(8), 2047.0, OP.subtract, cc(9), OP.mult)
-        TT(cc(26), cc(25), B1I, OP.add)
-        TS(E0, A("nb2"), cc(25), OP.is_gt, RD, OP.mult)
-        TT(A("y1"), A("bs"), E0, OP.subtract)
-        TS(E2, A("ntm"), cc(24), OP.is_gt, cc(26), OP.mult)
-        TS(A("g2"), A("nb2"), cc(24), OP.is_gt, cc(26), OP.mult)
-        TT(E2, A("g2"), E2, OP.subtract)
-        TT(A("sf"), A("y1"), E2, OP.subtract)
-        CP(A("ls"), A("sf"))
+        MM(A("z2", 0, NC), [(A("idh"), A("ma")), (A("idi"), A("mb"))])
+        ACT(TA, AC, AF.Identity, C2049, 2.0)
+        ACT(BS, TA, AF.Identity, BA, INV)
+        ACT(A("rn"), A("nt"), AF.Identity, BS, SL)
+        ACT(RD, BA, AF.Copy, None, NIN)
+        TT(A("gm"), A("rn"), A("z2", 0, NC), OP.mult)
+        SF, DW = A("z0", 0, NC), A("pk2", 0, 2)
+        MM(SF, [(A("id16"), A("nt16")), (A("idnf"), A("gm"))], True, False)
+        MM(DW, [(A("idnf"), A("def", 0, 2))], True, False)
+        TS(A("na"), A("nt16"), AC, OP.subtract)
+        TS(A("nb"), A("nt16"), AC, OP.subtract, BC, OP.add)
+        TS(A("l1", 0, 1), BC, ODD, OP.mult, AC, OP.max)
+        ACT(A("nc"), IND(A(X, 0, P), A("l1", 0, 1)), AF.Copy)
+        TS(A("l1", 2, 3), FIRST, AC, OP.mult, SX, OP.add)
+        ACT(cc(28), A("nc", 0, 1), AF.Identity, CQ, CMH2)
+        ACT(A("nm", 0, 1), A("nc", 1, 2), AF.Identity, cc(28), MH)
+        ACT(A("nd", 0, 1), A("nm", 0, 1), AF.Identity, CM129)
+        CP(IND(A(X), A("l1", 2, 3)), A("nd"))
+        if t < RO - 1:
+            ACT(A("upd", 16 * t, 16 * t + 1), A("nm", 0, 1), AF.Identity, CM129)
+            send_new(t)
+        TS(MK, K2, K3, OP.is_equal)
+        TS(HI, ii(5), Q2, OP.max)
+        TS(LO, ii(5), Q2, OP.min, B1I, OP.add)
+        TS(MV, HI, BC, OP.is_gt, MK, OP.mult)
+        TS(ss(4), HI, 2047.0, OP.subtract, MV, OP.mult)
+        TS(ss(5), HI, LO, OP.subtract, MV, OP.mult)
+        MM(DW, [(A("grp16"), A("s", 4, 6))], False, True)
+        D, DC = A("pk2", 0, 1), A("pk2", 1, 2)
+        TS(A("ta"), A("nt16"), D, OP.is_gt, DC, OP.mult)
+        TS(A("tb"), A("nb"), D, OP.is_gt, DC, OP.mult)
+        TS(A("tc"), A("na"), DC, OP.is_gt, RD, OP.mult)
+        MM(SF, [(A("id16"), A("ta")), (A("idm16"), A("tb")), (A("idm16"), A("tc"))], False, True)
+        CP(A("ls"), SF)
         Y = "yb" if t == RO - 1 else XN
-        for k in (0, 1):
-            CP(A(Y, 512 * k, 512 * k + 512), IND(A(X, 0, 2 * P), A("ls", 32 * k, 32 * k + 32)))
-            ACT(A(Y, 1024 + 512 * k, 1536 + 512 * k), IND(A(X, 0, 2 * P), A("ls", 64 + 32 * k, 96 + 32 * k)), AF.Copy)
+        for k in range(4):
+            COPY(A(Y, 512 * k, 512 * k + 512), IND(A(X, 0, 2 * P), A("ls", 32 * k, 32 * k + 32)), k in RAV)
         if t == RO - 1:
             for k in range(4):
-                DMA("ysys"[k], H(T.y[:, 512 * k:512 * k + 512]), A("yb", 512 * k, 512 * k + 512), "dy%d" % k)
+                DMA("yyys"[k], H(T.y[:, 512 * k:512 * k + 512]), A("yb", 512 * k, 512 * k + 512), "dy%d" % k)
 
     for t in range(RO):
         one_round(t)
 
     n = len(ops)
-    post, left, tail = [[] for _ in ops], [len(o["pre"]) for o in ops], [0.0] * n
+    pre, post, tail = [o["pre"] for o in ops], [[] for _ in ops], [0.0] * n
     for i in range(n - 1, -1, -1):
-        o = ops[i]
-        for j in o["pre"]: post[j].append(i)
-        tail[i] = o["cost"] + o["lat"] + WAKE + max([tail[j] for j in post[i]] + [0.0])
+        for j in pre[i]: post[j].append(i)
+        tail[i] = ops[i]["cost"] + ops[i]["lat"] + WAKE + max([tail[j] for j in post[i]] + [0.0])
     pri = list(tail)
     for i in range(n - 1, -1, -1): pri[i] = max([tail[i] + ops[i]["bon"]] + [pri[j] + ops[i]["cost"] for j in post[i]])
-    ready, free, at, order = {}, {}, [0.0] * n, []
-    for i in range(n):
-        if not left[i]: ready.setdefault(ops[i]["q"], []).append(i)
-    while len(order) < n:
-        best = None
-        for q in sorted(ready):
-            if ready[q]:
-                st = lambda i: at[i] if q == "x" else max(at[i], free.get(q, 0.0))
-                s0 = min(st(i) for i in ready[q])
-                i = max([i for i in ready[q] if st(i) <= s0 + .05], key=lambda i: (pri[i], -i))
-                if best is None or st(i) < best[0]: best = (st(i), q, i)
-        s0, q, i = best
-        ready[q].remove(i)
-        order.append(i)
-        free[q] = s0 + ops[i]["cost"]
-        for j in post[i]:
-            at[j] = max(at[j], free[q] + ops[i]["lat"] + WAKE)
-            left[j] -= 1
-            if not left[j]: ready.setdefault(ops[j]["q"], []).append(j)
+
+    def place(seq, before, back):
+        at, S, E = [0.0] * n, {}, {}
+        for i in seq:
+            o = ops[i]
+            c, s, e = o["cost"], S.setdefault(o["q"], []), E.setdefault(o["q"], [])
+            t = max([at[j] + ops[j]["cost"] + (o if back else ops[j])["lat"] + WAKE for j in before[i]] + [0.0])
+            if o["q"] != "x":
+                k = len(s)
+                while k and e[k - 1] > t: k -= 1
+                while k < len(s) and t + c > s[k] + 1e-9:
+                    t = max(t, e[k])
+                    k += 1
+                s.insert(k, t); e.insert(k, t + c)
+            at[i] = t
+        return at
+
+    at = place(sorted(range(n), key=lambda i: (-pri[i], i)), pre, False)
+    best = (1e9, None)
+    for _ in range(PASSES):
+        span = max(at[i] + ops[i]["cost"] + ops[i]["lat"] for i in range(n))
+        if span < best[0]: best = (span, at)
+        back = place(sorted(range(n), key=lambda i: (-at[i] - ops[i]["cost"], -i)), post, True)
+        at = place(sorted(range(n), key=lambda i: (-back[i] - ops[i]["cost"], i)), pre, False)
+    order = sorted(range(n), key=lambda i: (best[1][i], i))
 
     clk, total, evs = {q: {} for q in list(Q) + ["x"]}, dict(arrived), {}
     for i in order:

@@ -3,26 +3,29 @@ from concourse.mybir import AluOpType, AxisListType, ActivationFunctionType
 
 OP, AF = AluOpType, ActivationFunctionType
 P, TW, M, RO, NR = 2048, 2048, 3, 5, 4
-NC, W = P // 16, 64
+NC = P // 16
+CH = [(0, 64), (64, 64)]
 SM = [0, 1]
 MG = [[(0, 1), (1, 3)], [(0, 3)]]
-XQV, AGV, XFV, RAV = [1, 3], [1, 3], [0, 1], [0, 2]
-GB = 64
+XQV, AGV, XFV, RAV = [1, 3], [1, 3], [0], [0, 2]
+ROUND8 = float(2 ** 26 + 2 ** 24)
 SELF_D = 1920
 SPX = 2 * P
 BIG = float(2 ** 27)
 SENDS = {0: (1, 2, 3), 1: (1, 2, 3), 2: (1, 2), 3: (2,)}
-CY, GA, FIX, WAKE = .001, 1.3, .02, .1
-PE, BON, LATE, PASSES = [.0005], 1.0, 7.0, 8
+CY, GA, FIX, WAKE, PE = .001, 1.3, .02, .1, .00065
+LATE, LANDS, AHEAD = 7.0, 9.0, 1.0
+MODEL, TRIES = {}, 6000
 
 SCRATCH = {}
 for _d, _l in {
-    "float32": "idnf 128 xf 2048 cf 40 kmf 16 kmt 16 grp 128 m16 16 nt 128 v3 128 vmn 128 ku 384 nf 128 uv 128 uf 128 key 128 prd 128 prh 128 prk 128 "
+    "float32": "idnf 128 xf 2048 cf 40 kmf 16 grp 128 m16 16 nt 128 v3 128 vmn 128 ku 384 kmt 16 uv 128 uf 128 key 128 prd 128 prh 128 prk 128 "
                "rn 128 gm 128 dg 16 dg2 32 def 8 c 64 nc 16 upd 64 land 192",
-    "bfloat16": "xa 4112 xb 4112 tmo 2048 tb1 2064 tb2 2064 tb3 2064 xq 2048 ag 2048 az 2048 yb 2048 wb 144 mf 144 mz 144 ml 144 "
+    "bfloat16": "xa 4112 xb 4112 tmo 2048 tb1 2064 tb2 2064 tb3 2064 xq 2048 ag 2048 az 2048 yb 2048 wb 144 mf 144 mz 144 wk 8 iv 128 "
                 "xs 2048 as 2048 ic 144 ig 128 emn 128 idm 128 ma 128 mb 128 idn 128 idf 128 idj 128 idk 128 ids 128 id1 128 "
                 "id2 128 idu 128 idb 128 idh 128 idi 128 em 128 one 128 eqb 384 ido 128 nd 16 ru 128 rq 128 e0 128 e2 128 ib 128 nm 16",
-    "float16": "mn 6144 md 144 q16 384 id16 128 id8 128 idm16 128 grp16 128 nt16 128 na 128 nb 128 lod 128 ta 128 tb 128 tc 128 s 16",
+    "float16": "mn 6144 md 144 q16 384 id16 128 id8 128 idm16 128 grp16 128 nt16 128 na 128 nb 128 lod 128 ta 128 tb 128 tc 128 s 16 "
+               "f16 128 id8k 128",
     "int32": "ipart 4 ci 16 wti 4 kmi 16 t3 384 q3 384 vm 128 qs 128 b1 128 hp 128 hs 128 cii 16",
     "uint16": "l3 384 lq 128 lh 128 ls 128 l1 16"}.items():
     _w = _l.split()
@@ -41,7 +44,7 @@ def rank_program(g, core, T, topo):
         return
     Q = {"v": g.vector, "s": g.scalar, "p": g.tensor, "g": g, "y": g.sync}
     QS = {"v": "qv", "s": "qs", "p": "qp", "g": "qg"}
-    ops, wr, rd, bon = [], {}, {}, [0.0]
+    ops, wr, rd, bon, count, starts = [], {}, {}, ["start"], {}, []
 
     def A(n, a=0, b=None, st=1):
         b = T[n].shape[-1] if b is None else b
@@ -66,7 +69,8 @@ def rank_program(g, core, T, topo):
                 wr[n], rd[n] = [], []
             (wr if k else rd)[n].append((a, b, q, me))
         pre.discard(me)
-        ops.append(dict(q=q, fn=fn, pre=sorted(pre), cost=cost, bon=bon[0], sem=sem, inc=inc, lat=lat, ev=ev))
+        count[bon[0]] = count.get(bon[0], 0) + 1
+        ops.append(dict(q=q, fn=fn, pre=sorted(pre), cost=cost, sig=(len(starts), bon[0], count[bon[0]]), sem=sem, inc=inc, lat=lat, ev=ev))
         return me
 
     def vcost(o, ins, two=False, half=False):
@@ -110,16 +114,16 @@ def rank_program(g, core, T, topo):
         if vec: CP(o, x)
         else: ACT(o, x, AF.Copy)
 
-    def MM(o, pairs, start=True, stop=True):
+    def MM(o, pairs, start=True, stop=True, each=False):
         def go():
             for i, z in enumerate(pairs):
-                k = g.tensor.matmul((z[2] if len(z) > 2 else o)[0], z[0][0], z[1][0], start and i == 0, stop and i == len(pairs) - 1)
+                k = g.tensor.matmul((z[2] if len(z) > 2 else o)[0], z[0][0], z[1][0], each or (start and i == 0), each or (stop and i == len(pairs) - 1))
             return k
-        f = [max(64, z[1][2]) * PE[0] * (4 if SCRATCH[z[0][1][0][0]][2] == "float32" else 1) for z in pairs]
+        f = [max(64, z[1][2]) * PE * (4 if SCRATCH[z[0][1][0][0]][2] == "float32" else 1) for z in pairs]
         note("p", go, [o], [y for z in pairs for y in z[:2]], sum(f), lat=.06)
 
     def DMA(q, o, x, sem):
-        note(q, lambda: Q[q].dma_start(o[0], x[0]), [o], [x], .1, sem, 16, 4.0)
+        note(q, lambda: Q[q].dma_start(o[0], x[0]), [o], [x], .1, sem, 16, 2.2 + max(o[2], x[2]) / 600)
 
     def SUMS(mat, buf, base, n):
         return [(A(mat, 15 - jj, 143 - jj), A(buf, base + jj, base + 16 * n, 16)) for jj in range(16)]
@@ -141,15 +145,17 @@ def rank_program(g, core, T, topo):
     IOTA([[1, 144]], A("ic"), 0)
     IOTA([[1, 8], [0, 16]], A("ig"), 0)
     C = lambda i: A("cf", i, i + 1)
-    (JJ, GK, IPF, F15, R15, FIRST, NF, ODD, MH, SX, ST, CW, CMD, CMF, CMZ, CML, CJ, CK, G15, CMH2, CMFN,
-     CR, CQ, CM129, C1, CM1, CM2, CMH, C2049, C2047, CB5) = [C(i) for i in range(31)]
+    (JJ, GK, IPF, F15, R15, FIRST, NF, ODD, MH, SX, ST, CW, CMD, CMF, CMZ, CJ, CK, G15, CMH2,
+     CR, CQ, CM129, C1, CM1, CMH, C2049, CB5) = [C(i) for i in range(27)]
     TS(A("ci", 0, 1), A("ipart", 0, 1), 15, OP.bitwise_and)
     TS(A("ci", 1, 2), A("ipart", 0, 1), 4, OP.arith_shift_right)
     TS(A("ci", 2, 3), A("ipart", 0, 1), 1, OP.bitwise_and)
     CP(JJ, A("ci", 0, 1)); CP(GK, A("ci", 1, 2)); CP(ODD, A("ci", 2, 3)); CP(IPF, A("ipart", 0, 1))
-    for b, v in ((CR, 2.0 ** -13 - .5), (CQ, 128.75), (CM129, -129.0), (C1, 1.0), (CM1, -1.0), (CM2, -8192.0 * SELF_D), (CMH, -.5), (C2049, 2049.0),
-                 (CB5, -4096.5), (A("one"), 1.0), (A("nd"), 0.0), (A("upd"), 0.0), (A("def", 0, 1), 2047.0), (A("dg2", 16, 17), 1.5 * 2 ** 22)):
+    for b, v in ((C1, 1.0), (A("one"), 1.0), (A("nd"), 0.0), (A("upd"), 0.0)):
         FILL(b, v)
+    for b, v in ((CR, 2.0 ** -13 - .5), (CQ, 128.75), (CM129, -129.0), (CM1, -1.0), (CMH, -.5), (C2049, 2049.0), (CB5, -4096.5),
+                 (A("def", 0, 1), 2047.0), (A("dg2", 16, 17), 1.5 * 2 ** 22)):
+        ACT(b, C1, AF.Copy, None, v)
     TS(G15, A("ci", 1, 2), 16.0, OP.mult, 15.0, OP.add)
     TS(F15, A("ci", 0, 1), 15.0, OP.is_lt)
     TS(R15, A("ci", 0, 1), 15.0, OP.is_equal)
@@ -160,13 +166,12 @@ def rank_program(g, core, T, topo):
     TS(CMZ, F15, 8188.0, OP.mult, 4.0, OP.add)
     TS(CJ, F15, 2.0, OP.mult, -1.0, OP.add)
     ACT(CMF, F15, AF.Copy, None, 8192.0)
-    ACT(CML, R15, AF.Copy, None, -4096.0)
     ACT(CK, F15, AF.Copy, None, -2.0)
     ACT(MH, F15, AF.Copy, None, .5)
     ACT(CMH2, MH, AF.Identity, C1, -1.0)
     TS(SX, JJ, float(SPX), OP.add, NF, OP.mult)
     TS(ST, JJ, float(TW), OP.add, NF, OP.mult)
-    for m, cw in (("wb", CW), ("md", CMD), ("mf", CMF), ("mz", CMZ), ("ml", CML)):
+    for m, cw in (("wb", CW), ("md", CMD), ("mf", CMF), ("mz", CMZ)):
         TS(A(m), A("ic"), G15, OP.is_equal, cw, OP.mult)
     IC = A("ic", 0, 128)
     TS(A("idn"), IC, IPF, OP.is_equal)
@@ -179,27 +184,36 @@ def rank_program(g, core, T, topo):
     TT(A("kmt", 0, 15), A("kmt", 0, 15), A("kmi", 0, 15), OP.add)
     TS(A("kmf", 0, 15), A("kmt", 0, 15), -32768.0, OP.mult)
     TS(A("kmt", 0, 15), A("kmf", 0, 15), .5, OP.mult)
+    TS(A("wk"), A("ic", 0, 8), GK, OP.is_equal, F15, OP.mult)
     TS(A("nt"), IC, 16.0, OP.mult, JJ, OP.add)
     TS(A("nt16"), IC, 16.0, OP.mult, JJ, OP.add)
-    for m, v in (("id16", 1.0), ("id8", 8.0), ("idm16", -1.0)):
+    for m, v in (("id16", 1.0), ("id8", 8.0), ("idm16", -1.0), ("id8k", 8192.0)):
         TS(A(m), IC, IPF, OP.is_equal, v, OP.mult)
     for m, v in (("idu", 129.0), ("idm", -1.0), ("ids", SELF_D * 16384.0), ("ido", SELF_D * -8192.0), ("id1", 2048.0), ("id2", 4096.0), ("idj", CJ),
                  ("idk", CK), ("idnf", 1.0), ("idb", BIG), ("idh", .5), ("idi", -.5)):
         ACT(A(m), A("idn"), AF.Copy, None, v)
     TS(A("m16"), A("ic", 0, 16), JJ, OP.is_equal)
-    for i in (0, 1):
-        for m in range(M):
-            MM(A("ps0", 192 * i + W * m, 192 * i + W * m + W), [(A("id16"), A("nt16", W * i, W * i + W))])
+    for c0, n in CH:
+        for m in range(M): CP(A("ps0", 3 * c0 + n * m, 3 * c0 + n * m + n), A("nt16", c0, c0 + n))
 
     sent, arrived = [0], {}
+
+    def shares(r, far):
+        src, dst = cores[r], {o: cores[(r - o) % NR] for o in range(1, NR)}
+        away = [o for o in far if dst[o] not in topo.cores_of(src)]
+        off = [topo.engines(src, c) for c in dst.values() if c not in topo.cores_of(src)][0]
+        es = {o: off[i * len(off) // len(away):(i + 1) * len(off) // len(away)] for i, o in enumerate(away)}
+        for o in far:
+            if o not in es: es[o] = [e for e in topo.engines(src, dst[o]) if e not in off]
+        return es
 
     def send_table(o):
         d = cores[(rank - o) % NR]
         rid, pid = topo.addr(d, core)
-        sent[0] += len(topo.engines(core, d))
-        arrived["tma%d" % o] = len(topo.engines(cores[(rank + o) % NR], core))
-        k = note("g", lambda: g.remote_dma(T["tb%d" % o][:, 0:TW], T.tmo[:], T.sem["tma%d" % o], T.sem.ls, pid, rid, topo.mask(core, d)),
-                 [], [A("tmo")], .5, None)
+        sent[0] += len(shares(rank, (o,))[o])
+        arrived["tma%d" % o] = len(shares((rank + o) % NR, (o,))[o])
+        k = note("g", lambda: g.remote_dma(T["tb%d" % o][:, 0:TW], T.tmo[:], T.sem["tma%d" % o], T.sem.ls, pid, rid,
+                                           sum(1 << e for e in shares(rank, (o,))[o])), [], [A("tmo")], .5, None)
         note("x", None, [A("tb%d" % o, 0, TW)], [], 0, None, 1, 4.0 + 6 * o, ("tma%d" % o, arrived["tma%d" % o]), (k,))
     for o in (1, 2, 3): send_table(o)
 
@@ -218,18 +232,8 @@ def rank_program(g, core, T, topo):
                 TS(L, A("land", 16 * k + 1, 16 * k + 2), FIRST, OP.mult, ST, OP.add)
                 CP(IND(A("tb%d" % o), L), A("land", 16 * k, 16 * k + 16))
 
-    def shares(r, t):
-        src, dst = cores[r], {o: cores[(r - o) % NR] for o in SENDS[t]}
-        away = [o for o in SENDS[t] if dst[o] not in topo.cores_of(src)]
-        off = topo.engines(src, dst[away[0]])
-        w = len(off) // len(away)
-        es = {o: off[i * w:i * w + w] for i, o in enumerate(away)}
-        for o in SENDS[t]:
-            if o not in es: es[o] = [e for e in topo.engines(src, dst[o]) if e not in off]
-        return es
-
     def send_new(t):
-        es, xs = shares(rank, t), []
+        es, xs = shares(rank, SENDS[t]), []
         for o in SENDS[t]:
             rid, pid = topo.addr(cores[(rank - o) % NR], core)
             k = len(landed)
@@ -238,7 +242,7 @@ def rank_program(g, core, T, topo):
                                         remote_sem=T.sem["ua%d_%d" % (t, o)], src=T.upd[:, 16 * t:16 * t + 16],
                                         dst=T.land[:, 16 * k:16 * k + 16]))
             sent[0] += len(es[o])
-            arrived["ua%d_%d" % (t, o)] = len(shares((rank + o) % NR, t)[o])
+            arrived["ua%d_%d" % (t, o)] = len(shares((rank + o) % NR, SENDS[t])[o])
         me = note("g", lambda: g.remote_dma_fused(xs, local_sem=T.sem.ls), [], [A("upd", 16 * t, 16 * t + 16)], .5, None)
         for o in SENDS[t]:
             k, s = landed[(t, o)], "ua%d_%d" % (t, o)
@@ -247,112 +251,111 @@ def rank_program(g, core, T, topo):
     def one_round(t):
         X, XN = ("xa", "xb") if t % 2 == 0 else ("xb", "xa")
         TB = "tb%d" % (1 + t % 3)
-        ONE = A("one", 0, W)
-        ch = lambda n, i, off=0: A(n, off + W * i, off + W * i + W)
-        c3 = lambda n, i, m0, m1: A(n, 192 * i + W * m0, 192 * i + W * m1)
-
-        def weighted(out, o, buf, i, r):
-            MM(o, SUMS("wb", buf, 16 * W * i, W) + [(A("idu"), ONE)])
-            ACT(r, o, AF.Identity, CR)
-            TT(out, r, o, OP.subtract)
+        ch = lambda n, i, off=0: A(n, off + CH[i][0], off + CH[i][0] + CH[i][1])
+        c3 = lambda n, i, m0, m1, k=1: A(n, k * (3 * CH[i][0] + CH[i][1] * m0), k * (3 * CH[i][0] + CH[i][1] * m1))
 
         def lists(i):
-            u, sq = ch("uv", i), ch("pq", i)
-            weighted(u, A("pu" if i == 0 else "pk2", 0, W), X, i, ch("ru", i))
+            c0, n = CH[i]
+            o, u, sq = A(["pu", "pk2"][i], 0, n), ch("uv", i), ch("pq", i)
+            bon[0] = "sums%d" % i
+            MM(o, [(A("idu"), A("one", 0, n))], True, False)
+            MM(o, SUMS("wb", X, 16 * c0, n), False, True)
+            ACT(ch("ru", i), o, AF.Identity, CR)
+            TT(u, ch("ru", i), o, OP.subtract)
             ACT(sq, u, AF.Square, None, 2048.0)
-            for m in range(M):
-                ACT(c3("ku", i, m, m + 1), u, AF.Identity, A("kmt", 3 * t + m, 3 * t + m + 1), A("kmf", 3 * t + m, 3 * t + m + 1))
-            ACT(ch("uf", i), u, AF.Copy, None, 2.0 ** 24)
             for m0, m1 in MG[i]:
                 for m in range(m0, m1):
+                    ACT(c3("ku", i, m, m + 1), u, AF.Identity, A("kmt", 3 * t + m, 3 * t + m + 1), A("kmf", 3 * t + m, 3 * t + m + 1))
                     TT(c3("t3", i, m, m + 1), c3("ku", i, m, m + 1), sq, OP.add)
                 TS(c3("q3", i, m0, m1), c3("t3", i, m0, m1), 3, OP.arith_shift_right, P - 1, OP.bitwise_and)
                 CP(c3("l3", i, m0, m1), c3("q3", i, m0, m1))
             TT(c3("eqb", i, 0, M), c3("q3", i, 0, M), c3("ps0", i, 0, M), OP.is_equal)
             CP(c3("q16", i, 0, M), c3("l3", i, 0, M))
+            ACT(ch("uf", i), u, AF.Copy, None, 2.0 ** 24)
+
+        def features():
+            bon[0] = "features"
+            MM(A("pu", NC, 2 * NC), [(A(X, jj, P, 16), A("wk"), A("pu", NC + jj, 2 * NC, 16)) for jj in range(16)], each=True)
+            TS(A("f16"), A("pu", NC, 2 * NC), float(SELF_D), OP.subtract)
 
         def pick(out, tab, lst, i, vec):
-            for k in (2 * i, 2 * i + 1):
-                COPY(A(out, 512 * k, 512 * k + 512), IND(A(tab, 0, P), A(lst, 32 * k, 32 * k + 32)), k in vec)
+            c0, n = CH[i]
+            for k, (a, b) in enumerate(((c0, c0 + n // 2), (c0 + n // 2, c0 + n))):
+                COPY(A(out, 16 * a, 16 * b), IND(A(tab, 0, P), A(lst, a, b)), 2 * i + k in vec)
 
         def near(i):
-            a, n = 16 * W * i, W
-            o0, o1, o2 = A("pk1", 0, n), A("pk1", n, 2 * n), A("pk2", 0, n)
-            for m in range(2 if i in SM else 3):
-                for h in range(0, n, GB):
-                    TT(A("mn", 3 * a + 16 * (n * m + h), 3 * a + 16 * (n * m + h + GB)),
-                       IND(A("xf"), A("l3", 192 * i + n * m + h, 192 * i + n * m + h + GB)), A(X, a + 16 * h, a + 16 * (h + GB)), OP.min)
-            low = lambda m: [(A("ids"), c3("eqb", i, m, m + 1)), (A("id16"), c3("q16", i, m, m + 1))] + ([(A("id%d" % m), ONE)] if m else [])
-            mins = lambda m: SUMS("md", "mn", 3 * a + 16 * n * m, n) + [(A("idnf"), ch("nf", i))] + low(m)
-            MM(o0, mins(0))
-            ACT(ch("v3", i), o0, AF.Copy)
-            MM(o1, mins(1))
-            if i in SM:
-                for k, p0 in enumerate(range(a, a + 16 * n, 512)):
-                    w, l0 = A("z%d" % (2 - k)), 192 * i + 2 * n + 32 * k
-                    ACT(A("xs", p0, p0 + 512), IND(A(X, 0, P), A("l3", l0, l0 + 32)), AF.Copy)
-                    MM(w, [(A("idm"), A(X, p0, p0 + 512)), (A("idn"), A("xs", p0, p0 + 512))])
-                    ACT(A("as", p0, p0 + 512), w, AF.Abs)
-                MM(o2, SUMS("mf", "as", a, n) + [(A("ido"), ONE)] + low(2))
-            else:
-                MM(o2, mins(2))
-            TT(ch("vmn", i), ch("v3", i), o1, OP.min)
-            TT(ch("vm", i), ch("vmn", i), o2, OP.min)
+            c0, n = CH[i]
+            a, one = 16 * c0, A("one", 0, n)
+            o = [A("pk1", 0, n), A("pk1", n, 2 * n), A("pk2", 0, n)]
+            bon[0] = "near%d" % i
+            for m in range(M):
+                low = [(A("id16"), c3("q16", i, m, m + 1))] + ([(A("id%d" % m), one)] if m else [])
+                if m < 2 or i not in SM:
+                    TT(c3("mn", i, m, m + 1, 16), IND(A("xf"), c3("l3", i, m, m + 1)), A(X, a, a + 16 * n), OP.min)
+                    MM(o[m], [(A("f16"), ch("id8k", i))] + low, True, False)
+                    MM(o[m], SUMS("md", "mn", 3 * a + 16 * n * m, n) + [(A("ids"), c3("eqb", i, m, m + 1))], False, True)
+                else:
+                    MM(o[m], [(A("ido"), one)] + low, True, False)
+                    for k, p0 in enumerate(range(a, a + 16 * n, 512)):
+                        p1 = min(p0 + 512, a + 16 * n)
+                        w, l0 = A("z%d" % (2 - k), 0, p1 - p0), 3 * c0 + 2 * n + 32 * k
+                        ACT(A("xs", p0, p1), IND(A(X, 0, P), A("l3", l0, l0 + (p1 - p0) // 16)), AF.Copy)
+                        MM(w, [(A("idm"), A(X, p0, p1))], True, False)
+                        MM(w, [(A("idn"), A("xs", p0, p1))], False, True)
+                        ACT(A("as", p0, p1), w, AF.Abs)
+                    MM(o[m], SUMS("mf", "as", a, n) + [(A("ids"), c3("eqb", i, m, m + 1))], False, True)
+                if m == 0: ACT(ch("v3", i), o[0], AF.Copy)
+            TT(ch("vmn", i), ch("v3", i), o[1], OP.min)
+            TT(ch("vm", i), ch("vmn", i), o[2], OP.min)
             TS(ch("qs", i), ch("vm", i), P - 1, OP.bitwise_and)
             CP(ch("lq", i), ch("qs", i))
             TS(ch("b1", i), ch("vm", i), -8192, OP.bitwise_and)
 
         def asked(i):
+            c0, n = CH[i]
+            a, b, s = 16 * c0, 16 * (c0 + n), 2
+            bon[0] = "asked%d" % i
             pick("xq", X, "lq", i, XQV)
-            uq = ch("ps0", i, 384)
-            weighted(uq, A("pu", 0, W), "xq", i, ch("rq", i))
+            uq, o = ch("ps0", i, 384), A("pu", 0, n)
+            MM(o, [(A("idu"), A("one", 0, n))], True, False)
+            MM(o, SUMS("wb", "xq", a, n), False, True)
+            ACT(ch("rq", i), o, AF.Identity, CR)
+            TT(uq, ch("rq", i), o, OP.subtract)
             TT(ch("hp", i), ch("uf", i), uq, OP.mult)
             TS(ch("hs", i), ch("hp", i), 4, OP.arith_shift_right, TW - 1, OP.bitwise_and)
             CP(ch("lh", i), ch("hs", i))
-            sg = [(A("z%d" % (k % 3)), 512 * k, 512 * k + 512) for k in (2 * i, 2 * i + 1)]
-            for z, p0, p1 in sg:
-                MM(z, [(A("idj"), A(X, p0, p1))], True, False)
-                MM(z, [(A("idn"), A("xq", p0, p1))], False, False)
             pick("ag", TB, "lh", i, AGV)
-            for z, p0, p1 in sg:
-                MM(z, [(A("idk"), A("ag", p0, p1))], False, True)
-                ACT(A("az", p0, p1), z, AF.Abs)
-
-        def keyed(i):
-            o, l = ch("pq", i, 256), ch("pk1", i, 128)
-            MM(o, SUMS("mz", "az", 16 * W * i, W) + [(A("id8"), ch("nt16", i))])
+            o, r8, w = ch("pq", i, 256), ch("ps0", i, 384), (b - a) // s
+            MM(o, [(A("id8"), ch("nt16", i))], True, False)
+            for k in range(s):
+                z = A("z%d" % ((s * i + k) % 3), 0, w)
+                MM(z, [(A("idj"), A(X, a + k, b, s))], True, False)
+                MM(z, [(A("idn"), A("xq", a + k, b, s))], False, False)
+                MM(z, [(A("idk"), A("ag", a + k, b, s))], False, True)
+                ACT(A("az", a + k * w, a + k * w + w), z, AF.Abs)
+                MM(o, [(A("mz", 15 - jj, 143 - jj), A("az", a + k * w + jj // s, a + k * w + w, 16 // s)) for jj in range(k, 16, s)], False, k == s - 1)
             TT(ch("key", i), ch("b1", i), o, OP.add)
-            MM(l, SUMS("ml", "az", 16 * W * i, W) + [(A("id16"), ch("nt16", i))])
-            TT(ch("lod", i), ch("qs", i), l, OP.min)
+            TT(ch("lod", i), ch("qs", i), c3("ps0", i, 0, 1), OP.min)
+            TS(r8, ch("key", i), ROUND8, OP.add, ROUND8, OP.subtract)
+            TT(ch("iv", i), ch("key", i), r8, OP.not_equal)
 
-        for i in (0, 1):
-            bon[0] = BON * (2 - i)
-            lists(i)
-        bon[0] = BON * 2
+        for i in (0, 1): lists(i)
+        features()
+        bon[0] = "tables"
         for k in range(4):
             b = A(["z0", "z1", "z2", "pk1"][k])
             MM(b, [(A("em"), A(X, 512 * k, 512 * k + 512))])
             COPY(A("xf", 512 * k, 512 * k + 512), b, k in XFV)
-        bon[0] = 0.0
         for k in range(4):
             ACT(A(X, P + 512 * k, P + 512 * k + 512), A(X, 512 * k, 512 * k + 512), AF.Identity, R15, CJ)
-        bon[0] = BON * 2
-        MM(A("pu", 128, 256), SUMS("mf", X, 0, NC))
-        ACT(A("nf"), A("pu", 128, 256), AF.Identity, CM2)
+        bon[0] = "landed"
         updates(t)
-        for i in (0, 1):
-            bon[0] = BON * (2 - i)
-            near(i)
-        for i in (0, 1):
-            bon[0] = BON * (2 - i)
-            asked(i)
-        for i in (0, 1):
-            bon[0] = BON * (2 - i)
-            keyed(i)
-        bon[0] = 0.0
+        for i in (0, 1): near(i)
+        for i in (0, 1): asked(i)
+        bon[0] = "choice"
 
         K0, K1, Q0, H0, K2, K3, Q2, MK, HI, LO, MV, AC, BC, INV, NIN, NN, N2, NB, SL, BA, RD, BS, TA = [cc(i) for i in range(23)]
-        E, B1I = A("ps0", 384, 512), A("def", 1, 2)
+        E, B1I = A("pk1", 0, NC), A("def", 1, 2)
         KEY, KM = A("key"), A("z1", 0, NC)
         RED(K0, KEY, OP.min)
         TS(A("dg"), A("m16"), K0, OP.mult)
@@ -364,6 +367,7 @@ def rank_program(g, core, T, topo):
         TS(ss(0), K0, K1, OP.is_equal, Q0, OP.mult)
         MM(A("pu", 16, 17), [(A("grp16"), ss(0))])
         MM(KM, [(A("idnf"), KEY)], True, False)
+        MM(KM, [(A("idb"), A("iv"))], False, False)
         CP(ii(0), K1)
         TS(ii(1), ii(0), 3, OP.arith_shift_right, P - 1, OP.bitwise_and)
         TS(ii(2), ii(0), 4, OP.bitwise_and)
@@ -371,11 +375,13 @@ def rank_program(g, core, T, topo):
         TT(AC, ii(1), A("pu", 16, 17), OP.min)
         TT(BC, ii(1), A("pu", 16, 17), OP.max)
         if t < RO - 1:
+            bon[0] = "number"
             TT(A("prh"), A("hs"), E, OP.mult)
             RED(H0, A("prh"), OP.add)
             TS(ss(2), K0, K1, OP.is_equal, H0, OP.mult)
             MM(A("pq", 0, 1), [(A("grp16"), ss(2))])
             ACT(A("upd", 16 * t + 1, 16 * t + 2), A("pq", 0, 1), AF.Copy)
+            bon[0] = "choice"
         ACT(A("ib"), A("one"), AF.Copy, None, INV)
         TS(A("e0"), A("lod"), AC, OP.is_le)
         TS(A("e2"), A("lod"), BC, OP.is_ge)
@@ -419,8 +425,10 @@ def rank_program(g, core, T, topo):
         ACT(A("nd", 0, 1), A("nm", 0, 1), AF.Identity, CM129)
         CP(IND(A(X), A("l1", 2, 3)), A("nd"))
         if t < RO - 1:
+            bon[0] = "send"
             ACT(A("upd", 16 * t, 16 * t + 1), A("nm", 0, 1), AF.Identity, CM129)
             send_new(t)
+            bon[0] = "choice"
         TS(MK, K2, K3, OP.is_equal)
         TS(HI, ii(5), Q2, OP.max)
         TS(LO, ii(5), Q2, OP.min, B1I, OP.add)
@@ -433,6 +441,7 @@ def rank_program(g, core, T, topo):
         TS(A("tb"), A("nb"), D, OP.is_gt, DC, OP.mult)
         TS(A("tc"), A("na"), DC, OP.is_gt, RD, OP.mult)
         MM(SF, [(A("id16"), A("ta")), (A("idm16"), A("tb")), (A("idm16"), A("tc"))], False, True)
+        starts.append(len(ops)); count.clear(); bon[0] = "order"
         CP(A("ls"), SF)
         Y = "yb" if t == RO - 1 else XN
         for k in range(4):
@@ -444,21 +453,15 @@ def rank_program(g, core, T, topo):
     for t in range(RO):
         one_round(t)
 
-    n = len(ops)
-    pre, post, tail = [o["pre"] for o in ops], [[] for _ in ops], [0.0] * n
-    for i in range(n - 1, -1, -1):
-        for j in pre[i]: post[j].append(i)
-        tail[i] = ops[i]["cost"] + ops[i]["lat"] + WAKE + max([tail[j] for j in post[i]] + [0.0])
-    pri = list(tail)
-    for i in range(n - 1, -1, -1): pri[i] = max([tail[i] + ops[i]["bon"]] + [pri[j] + ops[i]["cost"] for j in post[i]])
-
     def place(seq, before, back):
-        at, S, E = [0.0] * n, {}, {}
+        at, S, E = {}, {}, {}
         for i in seq:
-            o = ops[i]
-            c, s, e = o["cost"], S.setdefault(o["q"], []), E.setdefault(o["q"], [])
-            t = max([at[j] + ops[j]["cost"] + (o if back else ops[j])["lat"] + WAKE for j in before[i]] + [0.0])
-            if o["q"] != "x":
+            q, c, t = ops[i]["q"], ops[i]["cost"], 0.0
+            s, e = S.setdefault(q, []), E.setdefault(q, [])
+            for j in before[i]:
+                if j in at: t = max(t, at[j] + ops[j]["cost"] + (1e-6 if q == ops[j]["q"] == "p" else ops[i if back else j]["lat"] + WAKE))
+                elif ops[j]["q"] == "x": t = max(t, LANDS)
+            if q != "x":
                 k = len(s)
                 while k and e[k - 1] > t: k -= 1
                 while k < len(s) and t + c > s[k] + 1e-9:
@@ -468,14 +471,43 @@ def rank_program(g, core, T, topo):
             at[i] = t
         return at
 
-    at = place(sorted(range(n), key=lambda i: (-pri[i], i)), pre, False)
-    best = (1e9, None)
-    for _ in range(PASSES):
-        span = max(at[i] + ops[i]["cost"] + ops[i]["lat"] for i in range(n))
-        if span < best[0]: best = (span, at)
-        back = place(sorted(range(n), key=lambda i: (-at[i] - ops[i]["cost"], -i)), post, True)
-        at = place(sorted(range(n), key=lambda i: (-back[i] - ops[i]["cost"], i)), pre, False)
-    order = sorted(range(n), key=lambda i: (best[1][i], i))
+    def settle(due, passes):
+        ids = sorted(due)
+        for i in ids[::-1]:
+            for j in post[i]:
+                if j in due and due[i] > due[j] - 1e-6: due[i] = due[j] - 1e-6
+        at = place(sorted(ids, key=lambda i: (due[i], i)), pre, False)
+        best = (max(at[i] + ends[i] for i in ends if i in at), at)
+        for _ in range(passes):
+            back = place(sorted(ids, key=lambda i: (-at[i] - ops[i]["cost"], -i)), post, True)
+            at = place(sorted(ids, key=lambda i: (-back[i] - ops[i]["cost"], i)), pre, False)
+            span = max(at[i] + ends[i] for i in ends if i in at)
+            if span <= best[0]: best = (span, at)
+        return best
+
+    n = len(ops)
+    pre, post, tail = [o["pre"] for o in ops], [[] for _ in ops], [0.0] * n
+    for i in range(n - 1, -1, -1):
+        for j in pre[i]: post[j].append(i)
+        tail[i] = ops[i]["cost"] + ops[i]["lat"] + WAKE + max([tail[j] for j in post[i]] + [0.0])
+    ends = {i: ops[i]["cost"] + ops[i]["lat"] for i in starts + list(range(n - 4, n))}
+    ends.update({i: AHEAD for i in range(n) if ops[i]["q"] == "g"})
+    if not MODEL:
+        ids, seed = list(range(starts[1], starts[2] + 1)), [1]
+
+        def chance():
+            seed[0] = (seed[0] * 1103515245 + 12345) % 2 ** 31
+            return seed[0] / 2 ** 31
+        best = cur = settle({i: -tail[i] for i in ids}, 1)
+        for k in range(TRIES):
+            due = dict(cur[1])
+            for _ in range(1 + int(3 * chance())): due[ids[int(len(ids) * chance())]] += 2 * (chance() + chance() + chance() - 1.5)
+            new = settle(due, 1)
+            if new[0] <= cur[0] + .2 * chance() * (1 - k / TRIES): cur = new
+            if new[0] < best[0]: best = new
+        MODEL.update({ops[i]["sig"][1:]: best[1][i] for i in ids[:-1]})
+    at = settle({i: 100.0 * ops[i]["sig"][0] + MODEL.get(ops[i]["sig"][1:], 99.0) for i in range(n)}, 0)[1]
+    order = sorted(range(n), key=lambda i: (at[i], i))
 
     clk, total, evs = {q: {} for q in list(Q) + ["x"]}, dict(arrived), {}
     for i in order:
@@ -484,7 +516,7 @@ def rank_program(g, core, T, topo):
             evs[i] = (o["ev"], {})
             continue
         for j in o["pre"]:
-            if evs[j] is not None:
+            if evs[j] is not None and not q == ops[j]["q"] == "p":
                 (s, v), snap = evs[j]
                 if clk[q].get(s, 0) < v and need.get(s, (0,))[0] < v: need[s] = (v, snap)
         items = sorted(need.items())

from concourse.bass import DstId, RemoteDMATransfer
from concourse.mybir import AluOpType, AxisListType, ActivationFunctionType

OP, AF = AluOpType, ActivationFunctionType
P, TW, M, RO, NR = 2048, 2048, 3, 5, 4
NC = P // 16
CH = [(0, 64), (64, 64)]
SM = [0, 1]
MG = [[(0, 1), (1, 3)], [(0, 3)]]
XQV, AGV, XFV, RAV = [1, 3], [1, 3], [0], [0, 2]
ROUND8 = float(2 ** 26 + 2 ** 24)
SELF_D = 1920
SPX = 2 * P
BIG = float(2 ** 27)
SENDS = {0: (1, 2, 3), 1: (1, 2, 3), 2: (1, 2), 3: (2,)}
CY, GA, FIX, WAKE, PE = .001, 1.3, .02, .1, .00065
LATE, LANDS, AHEAD = 7.0, 9.0, 1.0
MODEL, TRIES = {}, 6000

SCRATCH = {}
for _d, _l in {
    "float32": "idnf 128 xf 2048 cf 40 kmf 16 grp 128 m16 16 nt 128 v3 128 vmn 128 ku 384 kmt 16 uv 128 uf 128 key 128 prd 128 prh 128 prk 128 "
               "rn 128 gm 128 dg 16 dg2 32 def 8 c 64 nc 16 upd 64 land 192",
    "bfloat16": "xa 4112 xb 4112 tmo 2048 tb1 2064 tb2 2064 tb3 2064 xq 2048 ag 2048 az 2048 yb 2048 wb 144 mf 144 mz 144 wk 8 iv 128 "
                "xs 2048 as 2048 ic 144 ig 128 emn 128 idm 128 ma 128 mb 128 idn 128 idf 128 idj 128 idk 128 ids 128 id1 128 "
                "id2 128 idu 128 idb 128 idh 128 idi 128 em 128 one 128 eqb 384 ido 128 nd 16 ru 128 rq 128 e0 128 e2 128 ib 128 nm 16",
    "float16": "mn 6144 md 144 q16 384 id16 128 id8 128 idm16 128 grp16 128 nt16 128 na 128 nb 128 lod 128 ta 128 tb 128 tc 128 s 16 "
               "f16 128 id8k 128",
    "int32": "ipart 4 ci 16 wti 4 kmi 16 t3 384 q3 384 vm 128 qs 128 b1 128 hp 128 hs 128 cii 16",
    "uint16": "l3 384 lq 128 lh 128 ls 128 l1 16"}.items():
    _w = _l.split()
    for _i in range(0, len(_w), 2):
        SCRATCH[_w[_i]] = ("sbuf", [128, int(_w[_i + 1])], _d)
PSUMS = ["ps0", "pu", "pq", "pk1", "pk2", "z0", "z1", "z2"]
for _n in PSUMS:
    SCRATCH[_n] = ("psum", [128, 512], "float32")
SEMAPHORES = ["qv", "qs", "qp", "qg", "dx0", "dx1", "dw", "dk", "dt", "dy0", "dy1", "dy2", "dy3", "ls", "tma1", "tma2", "tma3"] + \
             ["ua%d_%d" % (t, o) for t in SENDS for o in SENDS[t]]


def rank_program(g, core, T, topo):
    rank, cores = T.rank_of(core), T.cores
    if rank is None:
        return
    Q = {"v": g.vector, "s": g.scalar, "p": g.tensor, "g": g, "y": g.sync}
    QS = {"v": "qv", "s": "qs", "p": "qp", "g": "qg"}
    ops, wr, rd, bon, count, starts = [], {}, {}, ["start"], {}, []

    def A(n, a=0, b=None, st=1):
        b = T[n].shape[-1] if b is None else b
        return (T[n][:, a:b] if st == 1 else T[n][:, a:b:st], [(n, a, b)], (b - a + st - 1) // st)

    def IND(w, o):
        return (w[0].indirect(o[0]), w[1] + o[1], -16 * o[2])

    def note(q, fn, outs, ins, cost, sem="", inc=1, lat=0.0, ev=None, after=()):
        me, pre = len(ops), set(after)
        R = [(r, 0) for o in ins for r in o[1]] + [(r, 1) for o in outs for r in o[1]]
        for (n, a, b), k in R:
            for d, w2 in ((wr, 1), (rd, 0)):
                for a2, b2, q2, i2 in d.setdefault(n, []):
                    if (n in PSUMS and (q2 != q or q == "p")) or (a < b2 and a2 < b and (k or w2)):
                        pre.add(i2)
        for (n, a, b), k in R:
            if k and n not in PSUMS:
                for d in (wr, rd):
                    d[n] = [x for x in d[n] if not (a <= x[0] and x[1] <= b)]
            if n in PSUMS and q == "p":
                wr[n], rd[n] = [], []
            (wr if k else rd)[n].append((a, b, q, me))
        pre.discard(me)
        count[bon[0]] = count.get(bon[0], 0) + 1
        ops.append(dict(q=q, fn=fn, pre=sorted(pre), cost=cost, sig=(len(starts), bon[0], count[bon[0]]), sem=sem, inc=inc, lat=lat, ev=ev))
        return me

    def vcost(o, ins, two=False, half=False):
        n = max([x[2] for x in ins] + [o[2]])
        for x in ins + [o]:
            if x[2] < 0: return -x[2] * CY * (GA if x is not o else 3) + .05
        ps = any(x[1][0][0] in PSUMS for x in ins)
        if two and not ps: n *= 2
        if half and not ps and all(SCRATCH.get(x[1][0][0], ("", "", ""))[2] in ("bfloat16", "float16", "uint16") for x in ins + [o]): n //= 2
        return max(64, n) * CY + FIX

    def TT(o, x, y, op):
        note("v", lambda: g.vector.tensor_tensor(o[0], x[0], y[0], op), [o], [x, y], vcost(o, [x, y], two=True))

    def TS(o, x, s1, op0, s2=None, op1=None):
        ins = [x] + [s for s in (s1, s2) if isinstance(s, tuple)]
        v1 = s1[0] if isinstance(s1, tuple) else s1
        v2 = s2[0] if isinstance(s2, tuple) else s2
        if op1 is None:
            note("v", lambda: g.vector.tensor_scalar(o[0], x[0], v1, None, op0), [o], ins, vcost(o, [x], half=True))
        else:
            note("v", lambda: g.vector.tensor_scalar(o[0], x[0], v1, v2, op0, op1), [o], ins, vcost(o, [x], half=True))

    def CP(o, x):
        note("v", lambda: g.vector.tensor_copy(o[0], x[0]), [o], [x], vcost(o, [x], half=True))

    def RED(o, x, op):
        note("v", lambda: g.vector.tensor_reduce(o[0], x[0], AxisListType.X, op), [o], [x], vcost(o, [x]))

    def FILL(o, v):
        note("v", lambda: g.vector.memset(o[0], v), [o], [], vcost(o, []))

    def ACT(o, x, func=AF.Copy, bias=None, scale=None):
        kw = {}
        if bias is not None: kw["bias"] = bias[0]
        if scale is not None: kw["scale"] = scale[0] if isinstance(scale, tuple) else scale
        note("s", lambda: g.scalar.activation(o[0], x[0], func, **kw), [o],
             [x] + [s for s in (bias, scale) if isinstance(s, tuple)], vcost(o, [x]) + .015)

    def COPY(o, x, vec):
        if vec: CP(o, x)
        else: ACT(o, x, AF.Copy)

    def MM(o, pairs, start=True, stop=True, each=False):
        def go():
            for i, z in enumerate(pairs):
                k = g.tensor.matmul((z[2] if len(z) > 2 else o)[0], z[0][0], z[1][0], each or (start and i == 0), each or (stop and i == len(pairs) - 1))
            return k
        f = [max(64, z[1][2]) * PE * (4 if SCRATCH[z[0][1][0][0]][2] == "float32" else 1) for z in pairs]
        note("p", go, [o], [y for z in pairs for y in z[:2]], sum(f), lat=.06)

    def DMA(q, o, x, sem):
        note(q, lambda: Q[q].dma_start(o[0], x[0]), [o], [x], .1, sem, 16, 2.2 + max(o[2], x[2]) / 600)

    def SUMS(mat, buf, base, n):
        return [(A(mat, 15 - jj, 143 - jj), A(buf, base + jj, base + 16 * n, 16)) for jj in range(16)]

    def IOTA(pattern, b, cm, small=True):
        kw = {"allow_small_or_imprecise_dtypes": True} if small else {}
        note("g", lambda: g.iota(b[0], pattern, 0, cm, **kw), [b], [], .13 + 2 * b[2] * CY)

    def H(ap):
        return (ap, [], 0)

    DMA("s", A("tmo"), H(T.tm[:]), "dt")
    DMA("y", A("wti", 0, 1), H(T.wt[:]), "dw")
    DMA("y", A("xa", 0, P // 2), H(T.x[:, 0:P // 2]), "dx0")
    DMA("y", A("xa", P // 2, P), H(T.x[:, P // 2:P]), "dx1")
    DMA("y", A("kmi", 0, 15), H(T.km[:]), "dk")

    IOTA([[0, 1]], A("ipart", 0, 1), 1, False)
    IOTA([[1, 144]], A("ic"), 0)
    IOTA([[1, 8], [0, 16]], A("ig"), 0)
    C = lambda i: A("cf", i, i + 1)
    (JJ, GK, IPF, F15, R15, FIRST, NF, ODD, MH, SX, ST, CW, CMD, CMF, CMZ, CJ, CK, G15, CMH2,
     CR, CQ, CM129, C1, CM1, CMH, C2049, CB5) = [C(i) for i in range(27)]
    TS(A("ci", 0, 1), A("ipart", 0, 1), 15, OP.bitwise_and)
    TS(A("ci", 1, 2), A("ipart", 0, 1), 4, OP.arith_shift_right)
    TS(A("ci", 2, 3), A("ipart", 0, 1), 1, OP.bitwise_and)
    CP(JJ, A("ci", 0, 1)); CP(GK, A("ci", 1, 2)); CP(ODD, A("ci", 2, 3)); CP(IPF, A("ipart", 0, 1))
    for b, v in ((C1, 1.0), (A("one"), 1.0), (A("nd"), 0.0), (A("upd"), 0.0)):
        FILL(b, v)
    for b, v in ((CR, 2.0 ** -13 - .5), (CQ, 128.75), (CM129, -129.0), (CM1, -1.0), (CMH, -.5), (C2049, 2049.0), (CB5, -4096.5),
                 (A("def", 0, 1), 2047.0), (A("dg2", 16, 17), 1.5 * 2 ** 22)):
        ACT(b, C1, AF.Copy, None, v)
    TS(G15, A("ci", 1, 2), 16.0, OP.mult, 15.0, OP.add)
    TS(F15, A("ci", 0, 1), 15.0, OP.is_lt)
    TS(R15, A("ci", 0, 1), 15.0, OP.is_equal)
    TS(FIRST, A("ci", 0, 1), 0.0, OP.is_equal)
    TS(NF, A("ci", 0, 1), 0.0, OP.is_gt)
    TS(CW, A("wti", 0, 1), 2.0 ** -12, OP.mult)
    TS(CMD, F15, -8192.0, OP.mult, -8192.0, OP.add)
    TS(CMZ, F15, 8188.0, OP.mult, 4.0, OP.add)
    TS(CJ, F15, 2.0, OP.mult, -1.0, OP.add)
    ACT(CMF, F15, AF.Copy, None, 8192.0)
    ACT(CK, F15, AF.Copy, None, -2.0)
    ACT(MH, F15, AF.Copy, None, .5)
    ACT(CMH2, MH, AF.Identity, C1, -1.0)
    TS(SX, JJ, float(SPX), OP.add, NF, OP.mult)
    TS(ST, JJ, float(TW), OP.add, NF, OP.mult)
    for m, cw in (("wb", CW), ("md", CMD), ("mf", CMF), ("mz", CMZ)):
        TS(A(m), A("ic"), G15, OP.is_equal, cw, OP.mult)
    IC = A("ic", 0, 128)
    TS(A("idn"), IC, IPF, OP.is_equal)
    TS(A("grp"), A("ig"), GK, OP.is_equal)
    TS(A("grp16"), A("ig"), GK, OP.is_equal)
    TS(A("emn"), IC, G15, OP.is_equal, F15, OP.mult)
    TS(A("idf"), IC, IPF, OP.is_equal, F15, OP.mult)
    TT(A("em"), A("idf"), A("emn"), OP.subtract)
    TS(A("kmt", 0, 15), A("kmi", 0, 15), 1024.0, OP.is_ge, -2048.0, OP.mult)
    TT(A("kmt", 0, 15), A("kmt", 0, 15), A("kmi", 0, 15), OP.add)
    TS(A("kmf", 0, 15), A("kmt", 0, 15), -32768.0, OP.mult)
    TS(A("kmt", 0, 15), A("kmf", 0, 15), .5, OP.mult)
    TS(A("wk"), A("ic", 0, 8), GK, OP.is_equal, F15, OP.mult)
    TS(A("nt"), IC, 16.0, OP.mult, JJ, OP.add)
    TS(A("nt16"), IC, 16.0, OP.mult, JJ, OP.add)
    for m, v in (("id16", 1.0), ("id8", 8.0), ("idm16", -1.0), ("id8k", 8192.0)):
        TS(A(m), IC, IPF, OP.is_equal, v, OP.mult)
    for m, v in (("idu", 129.0), ("idm", -1.0), ("ids", SELF_D * 16384.0), ("ido", SELF_D * -8192.0), ("id1", 2048.0), ("id2", 4096.0), ("idj", CJ),
                 ("idk", CK), ("idnf", 1.0), ("idb", BIG), ("idh", .5), ("idi", -.5)):
        ACT(A(m), A("idn"), AF.Copy, None, v)
    TS(A("m16"), A("ic", 0, 16), JJ, OP.is_equal)
    for c0, n in CH:
        for m in range(M): CP(A("ps0", 3 * c0 + n * m, 3 * c0 + n * m + n), A("nt16", c0, c0 + n))

    sent, arrived = [0], {}

    def shares(r, far):
        src, dst = cores[r], {o: cores[(r - o) % NR] for o in range(1, NR)}
        away = [o for o in far if dst[o] not in topo.cores_of(src)]
        off = [topo.engines(src, c) for c in dst.values() if c not in topo.cores_of(src)][0]
        es = {o: off[i * len(off) // len(away):(i + 1) * len(off) // len(away)] for i, o in enumerate(away)}
        for o in far:
            if o not in es: es[o] = [e for e in topo.engines(src, dst[o]) if e not in off]
        return es

    def send_table(o):
        d = cores[(rank - o) % NR]
        rid, pid = topo.addr(d, core)
        sent[0] += len(shares(rank, (o,))[o])
        arrived["tma%d" % o] = len(shares((rank + o) % NR, (o,))[o])
        k = note("g", lambda: g.remote_dma(T["tb%d" % o][:, 0:TW], T.tmo[:], T.sem["tma%d" % o], T.sem.ls, pid, rid,
                                           sum(1 << e for e in shares(rank, (o,))[o])), [], [A("tmo")], .5, None)
        note("x", None, [A("tb%d" % o, 0, TW)], [], 0, None, 1, 4.0 + 6 * o, ("tma%d" % o, arrived["tma%d" % o]), (k,))
    for o in (1, 2, 3): send_table(o)

    cc = lambda i: A("c", i, i + 1)
    ii = lambda i: A("cii", i, i + 1)
    ss = lambda i: A("s", i, i + 1)
    seen, landed = set(), {}

    def updates(t):
        o = 1 + t % 3
        for t0 in range(t):
            if (t0, o) in landed and (t0, o) not in seen:
                seen.add((t0, o))
                k = landed[(t0, o)]
                L = A("l1", 4 + 2 * (len(seen) % 2), 5 + 2 * (len(seen) % 2))
                TS(L, A("land", 16 * k + 1, 16 * k + 2), FIRST, OP.mult, ST, OP.add)
                CP(IND(A("tb%d" % o), L), A("land", 16 * k, 16 * k + 16))

    def send_new(t):
        es, xs = shares(rank, SENDS[t]), []
        for o in SENDS[t]:
            rid, pid = topo.addr(cores[(rank - o) % NR], core)
            k = len(landed)
            landed[(t, o)] = k
            xs.append(RemoteDMATransfer(dst_ids=[DstId(rid=rid, pnc=pid)], dma_engine_mask=sum(1 << e for e in es[o]),
                                        remote_sem=T.sem["ua%d_%d" % (t, o)], src=T.upd[:, 16 * t:16 * t + 16],
                                        dst=T.land[:, 16 * k:16 * k + 16]))
            sent[0] += len(es[o])
            arrived["ua%d_%d" % (t, o)] = len(shares((rank + o) % NR, SENDS[t])[o])
        me = note("g", lambda: g.remote_dma_fused(xs, local_sem=T.sem.ls), [], [A("upd", 16 * t, 16 * t + 16)], .5, None)
        for o in SENDS[t]:
            k, s = landed[(t, o)], "ua%d_%d" % (t, o)
            note("x", None, [A("land", 16 * k, 16 * k + 16)], [], 0, None, 1, LATE, (s, arrived[s]), (me,))

    def one_round(t):
        X, XN = ("xa", "xb") if t % 2 == 0 else ("xb", "xa")
        TB = "tb%d" % (1 + t % 3)
        ch = lambda n, i, off=0: A(n, off + CH[i][0], off + CH[i][0] + CH[i][1])
        c3 = lambda n, i, m0, m1, k=1: A(n, k * (3 * CH[i][0] + CH[i][1] * m0), k * (3 * CH[i][0] + CH[i][1] * m1))

        def lists(i):
            c0, n = CH[i]
            o, u, sq = A(["pu", "pk2"][i], 0, n), ch("uv", i), ch("pq", i)
            bon[0] = "sums%d" % i
            MM(o, [(A("idu"), A("one", 0, n))], True, False)
            MM(o, SUMS("wb", X, 16 * c0, n), False, True)
            ACT(ch("ru", i), o, AF.Identity, CR)
            TT(u, ch("ru", i), o, OP.subtract)
            ACT(sq, u, AF.Square, None, 2048.0)
            for m0, m1 in MG[i]:
                for m in range(m0, m1):
                    ACT(c3("ku", i, m, m + 1), u, AF.Identity, A("kmt", 3 * t + m, 3 * t + m + 1), A("kmf", 3 * t + m, 3 * t + m + 1))
                    TT(c3("t3", i, m, m + 1), c3("ku", i, m, m + 1), sq, OP.add)
                TS(c3("q3", i, m0, m1), c3("t3", i, m0, m1), 3, OP.arith_shift_right, P - 1, OP.bitwise_and)
                CP(c3("l3", i, m0, m1), c3("q3", i, m0, m1))
            TT(c3("eqb", i, 0, M), c3("q3", i, 0, M), c3("ps0", i, 0, M), OP.is_equal)
            CP(c3("q16", i, 0, M), c3("l3", i, 0, M))
            ACT(ch("uf", i), u, AF.Copy, None, 2.0 ** 24)

        def features():
            bon[0] = "features"
            MM(A("pu", NC, 2 * NC), [(A(X, jj, P, 16), A("wk"), A("pu", NC + jj, 2 * NC, 16)) for jj in range(16)], each=True)
            TS(A("f16"), A("pu", NC, 2 * NC), float(SELF_D), OP.subtract)

        def pick(out, tab, lst, i, vec):
            c0, n = CH[i]
            for k, (a, b) in enumerate(((c0, c0 + n // 2), (c0 + n // 2, c0 + n))):
                COPY(A(out, 16 * a, 16 * b), IND(A(tab, 0, P), A(lst, a, b)), 2 * i + k in vec)

        def near(i):
            c0, n = CH[i]
            a, one = 16 * c0, A("one", 0, n)
            o = [A("pk1", 0, n), A("pk1", n, 2 * n), A("pk2", 0, n)]
            bon[0] = "near%d" % i
            for m in range(M):
                low = [(A("id16"), c3("q16", i, m, m + 1))] + ([(A("id%d" % m), one)] if m else [])
                if m < 2 or i not in SM:
                    TT(c3("mn", i, m, m + 1, 16), IND(A("xf"), c3("l3", i, m, m + 1)), A(X, a, a + 16 * n), OP.min)
                    MM(o[m], [(A("f16"), ch("id8k", i))] + low, True, False)
                    MM(o[m], SUMS("md", "mn", 3 * a + 16 * n * m, n) + [(A("ids"), c3("eqb", i, m, m + 1))], False, True)
                else:
                    MM(o[m], [(A("ido"), one)] + low, True, False)
                    for k, p0 in enumerate(range(a, a + 16 * n, 512)):
                        p1 = min(p0 + 512, a + 16 * n)
                        w, l0 = A("z%d" % (2 - k), 0, p1 - p0), 3 * c0 + 2 * n + 32 * k
                        ACT(A("xs", p0, p1), IND(A(X, 0, P), A("l3", l0, l0 + (p1 - p0) // 16)), AF.Copy)
                        MM(w, [(A("idm"), A(X, p0, p1))], True, False)
                        MM(w, [(A("idn"), A("xs", p0, p1))], False, True)
                        ACT(A("as", p0, p1), w, AF.Abs)
                    MM(o[m], SUMS("mf", "as", a, n) + [(A("ids"), c3("eqb", i, m, m + 1))], False, True)
                if m == 0: ACT(ch("v3", i), o[0], AF.Copy)
            TT(ch("vmn", i), ch("v3", i), o[1], OP.min)
            TT(ch("vm", i), ch("vmn", i), o[2], OP.min)
            TS(ch("qs", i), ch("vm", i), P - 1, OP.bitwise_and)
            CP(ch("lq", i), ch("qs", i))
            TS(ch("b1", i), ch("vm", i), -8192, OP.bitwise_and)

        def asked(i):
            c0, n = CH[i]
            a, b, s = 16 * c0, 16 * (c0 + n), 2
            bon[0] = "asked%d" % i
            pick("xq", X, "lq", i, XQV)
            uq, o = ch("ps0", i, 384), A("pu", 0, n)
            MM(o, [(A("idu"), A("one", 0, n))], True, False)
            MM(o, SUMS("wb", "xq", a, n), False, True)
            ACT(ch("rq", i), o, AF.Identity, CR)
            TT(uq, ch("rq", i), o, OP.subtract)
            TT(ch("hp", i), ch("uf", i), uq, OP.mult)
            TS(ch("hs", i), ch("hp", i), 4, OP.arith_shift_right, TW - 1, OP.bitwise_and)
            CP(ch("lh", i), ch("hs", i))
            pick("ag", TB, "lh", i, AGV)
            o, r8, w = ch("pq", i, 256), ch("ps0", i, 384), (b - a) // s
            MM(o, [(A("id8"), ch("nt16", i))], True, False)
            for k in range(s):
                z = A("z%d" % ((s * i + k) % 3), 0, w)
                MM(z, [(A("idj"), A(X, a + k, b, s))], True, False)
                MM(z, [(A("idn"), A("xq", a + k, b, s))], False, False)
                MM(z, [(A("idk"), A("ag", a + k, b, s))], False, True)
                ACT(A("az", a + k * w, a + k * w + w), z, AF.Abs)
                MM(o, [(A("mz", 15 - jj, 143 - jj), A("az", a + k * w + jj // s, a + k * w + w, 16 // s)) for jj in range(k, 16, s)], False, k == s - 1)
            TT(ch("key", i), ch("b1", i), o, OP.add)
            TT(ch("lod", i), ch("qs", i), c3("ps0", i, 0, 1), OP.min)
            TS(r8, ch("key", i), ROUND8, OP.add, ROUND8, OP.subtract)
            TT(ch("iv", i), ch("key", i), r8, OP.not_equal)

        for i in (0, 1): lists(i)
        features()
        bon[0] = "tables"
        for k in range(4):
            b = A(["z0", "z1", "z2", "pk1"][k])
            MM(b, [(A("em"), A(X, 512 * k, 512 * k + 512))])
            COPY(A("xf", 512 * k, 512 * k + 512), b, k in XFV)
        for k in range(4):
            ACT(A(X, P + 512 * k, P + 512 * k + 512), A(X, 512 * k, 512 * k + 512), AF.Identity, R15, CJ)
        bon[0] = "landed"
        updates(t)
        for i in (0, 1): near(i)
        for i in (0, 1): asked(i)
        bon[0] = "choice"

        K0, K1, Q0, H0, K2, K3, Q2, MK, HI, LO, MV, AC, BC, INV, NIN, NN, N2, NB, SL, BA, RD, BS, TA = [cc(i) for i in range(23)]
        E, B1I = A("pk1", 0, NC), A("def", 1, 2)
        KEY, KM = A("key"), A("z1", 0, NC)
        RED(K0, KEY, OP.min)
        TS(A("dg"), A("m16"), K0, OP.mult)
        MM(A("pu", 0, 16), [(A("grp"), A("dg"))])
        TS(E, KEY, K0, OP.is_equal)
        TT(A("prd"), A("qs"), E, OP.mult)
        RED(K1, A("pu", 0, 16), OP.min)
        RED(Q0, A("prd"), OP.add)
        TS(ss(0), K0, K1, OP.is_equal, Q0, OP.mult)
        MM(A("pu", 16, 17), [(A("grp16"), ss(0))])
        MM(KM, [(A("idnf"), KEY)], True, False)
        MM(KM, [(A("idb"), A("iv"))], False, False)
        CP(ii(0), K1)
        TS(ii(1), ii(0), 3, OP.arith_shift_right, P - 1, OP.bitwise_and)
        TS(ii(2), ii(0), 4, OP.bitwise_and)
        TS(INV, ii(2), .25, OP.mult)
        TT(AC, ii(1), A("pu", 16, 17), OP.min)
        TT(BC, ii(1), A("pu", 16, 17), OP.max)
        if t < RO - 1:
            bon[0] = "number"
            TT(A("prh"), A("hs"), E, OP.mult)
            RED(H0, A("prh"), OP.add)
            TS(ss(2), K0, K1, OP.is_equal, H0, OP.mult)
            MM(A("pq", 0, 1), [(A("grp16"), ss(2))])
            ACT(A("upd", 16 * t + 1, 16 * t + 2), A("pq", 0, 1), AF.Copy)
            bon[0] = "choice"
        ACT(A("ib"), A("one"), AF.Copy, None, INV)
        TS(A("e0"), A("lod"), AC, OP.is_le)
        TS(A("e2"), A("lod"), BC, OP.is_ge)
        MM(KM, [(A("idb"), A("ib")), (A("idb"), A("e0")), (A("idb"), A("e2"))], False, True)
        RED(K2, KM, OP.min)
        TS(A("dg2", 0, 16), A("m16"), K2, OP.mult)
        MM(A("pu", 0, 17), [(A("grp"), A("dg2", 0, 17))])
        TS(E, KM, K2, OP.is_equal)
        TT(A("prk"), A("qs"), E, OP.mult)
        RED(K3, A("pu", 0, 17), OP.min)
        RED(Q2, A("prk"), OP.add)
        CP(ii(4), K2)
        TS(ii(5), ii(4), 3, OP.arith_shift_right, P - 1, OP.bitwise_and)
        ACT(NIN, INV, AF.Identity, C1, -1.0)
        ACT(NN, INV, AF.Identity, CM1)
        ACT(N2, NIN, AF.Copy, None, 2047.0)
        ACT(NB, INV, AF.Identity, CB5, 4096.0)
        ACT(SL, INV, AF.Copy, None, -2.0)
        ACT(B1I, BC, AF.Identity, N2, NN)
        ACT(BA, AC, AF.Identity, BC, -1.0)
        ACT(cc(30), AC, AF.Identity, CMH, -1.0)
        ACT(cc(31), BC, AF.Identity, NB, -1.0)
        ACT(A("ma"), A("nt"), AF.Sign, cc(30))
        ACT(A("mb"), A("nt"), AF.Sign, cc(31))
        MM(A("z2", 0, NC), [(A("idh"), A("ma")), (A("idi"), A("mb"))])
        ACT(TA, AC, AF.Identity, C2049, 2.0)
        ACT(BS, TA, AF.Identity, BA, INV)
        ACT(A("rn"), A("nt"), AF.Identity, BS, SL)
        ACT(RD, BA, AF.Copy, None, NIN)
        TT(A("gm"), A("rn"), A("z2", 0, NC), OP.mult)
        SF, DW = A("z0", 0, NC), A("pk2", 0, 2)
        MM(SF, [(A("id16"), A("nt16")), (A("idnf"), A("gm"))], True, False)
        MM(DW, [(A("idnf"), A("def", 0, 2))], True, False)
        TS(A("na"), A("nt16"), AC, OP.subtract)
        TS(A("nb"), A("nt16"), AC, OP.subtract, BC, OP.add)
        TS(A("l1", 0, 1), BC, ODD, OP.mult, AC, OP.max)
        ACT(A("nc"), IND(A(X, 0, P), A("l1", 0, 1)), AF.Copy)
        TS(A("l1", 2, 3), FIRST, AC, OP.mult, SX, OP.add)
        ACT(cc(28), A("nc", 0, 1), AF.Identity, CQ, CMH2)
        ACT(A("nm", 0, 1), A("nc", 1, 2), AF.Identity, cc(28), MH)
        ACT(A("nd", 0, 1), A("nm", 0, 1), AF.Identity, CM129)
        CP(IND(A(X), A("l1", 2, 3)), A("nd"))
        if t < RO - 1:
            bon[0] = "send"
            ACT(A("upd", 16 * t, 16 * t + 1), A("nm", 0, 1), AF.Identity, CM129)
            send_new(t)
            bon[0] = "choice"
        TS(MK, K2, K3, OP.is_equal)
        TS(HI, ii(5), Q2, OP.max)
        TS(LO, ii(5), Q2, OP.min, B1I, OP.add)
        TS(MV, HI, BC, OP.is_gt, MK, OP.mult)
        TS(ss(4), HI, 2047.0, OP.subtract, MV, OP.mult)
        TS(ss(5), HI, LO, OP.subtract, MV, OP.mult)
        MM(DW, [(A("grp16"), A("s", 4, 6))], False, True)
        D, DC = A("pk2", 0, 1), A("pk2", 1, 2)
        TS(A("ta"), A("nt16"), D, OP.is_gt, DC, OP.mult)
        TS(A("tb"), A("nb"), D, OP.is_gt, DC, OP.mult)
        TS(A("tc"), A("na"), DC, OP.is_gt, RD, OP.mult)
        MM(SF, [(A("id16"), A("ta")), (A("idm16"), A("tb")), (A("idm16"), A("tc"))], False, True)
        starts.append(len(ops)); count.clear(); bon[0] = "order"
        CP(A("ls"), SF)
        Y = "yb" if t == RO - 1 else XN
        for k in range(4):
            COPY(A(Y, 512 * k, 512 * k + 512), IND(A(X, 0, 2 * P), A("ls", 32 * k, 32 * k + 32)), k in RAV)
        if t == RO - 1:
            for k in range(4):
                DMA("yyys"[k], H(T.y[:, 512 * k:512 * k + 512]), A("yb", 512 * k, 512 * k + 512), "dy%d" % k)

    for t in range(RO):
        one_round(t)

    def place(seq, before, back):
        at, S, E = {}, {}, {}
        for i in seq:
            q, c, t = ops[i]["q"], ops[i]["cost"], 0.0
            s, e = S.setdefault(q, []), E.setdefault(q, [])
            for j in before[i]:
                if j in at: t = max(t, at[j] + ops[j]["cost"] + (1e-6 if q == ops[j]["q"] == "p" else ops[i if back else j]["lat"] + WAKE))
                elif ops[j]["q"] == "x": t = max(t, LANDS)
            if q != "x":
                k = len(s)
                while k and e[k - 1] > t: k -= 1
                while k < len(s) and t + c > s[k] + 1e-9:
                    t = max(t, e[k])
                    k += 1
                s.insert(k, t); e.insert(k, t + c)
            at[i] = t
        return at

    def settle(due, passes):
        ids = sorted(due)
        for i in ids[::-1]:
            for j in post[i]:
                if j in due and due[i] > due[j] - 1e-6: due[i] = due[j] - 1e-6
        at = place(sorted(ids, key=lambda i: (due[i], i)), pre, False)
        best = (max(at[i] + ends[i] for i in ends if i in at), at)
        for _ in range(passes):
            back = place(sorted(ids, key=lambda i: (-at[i] - ops[i]["cost"], -i)), post, True)
            at = place(sorted(ids, key=lambda i: (-back[i] - ops[i]["cost"], i)), pre, False)
            span = max(at[i] + ends[i] for i in ends if i in at)
            if span <= best[0]: best = (span, at)
        return best

    n = len(ops)
    pre, post, tail = [o["pre"] for o in ops], [[] for _ in ops], [0.0] * n
    for i in range(n - 1, -1, -1):
        for j in pre[i]: post[j].append(i)
        tail[i] = ops[i]["cost"] + ops[i]["lat"] + WAKE + max([tail[j] for j in post[i]] + [0.0])
    ends = {i: ops[i]["cost"] + ops[i]["lat"] for i in starts + list(range(n - 4, n))}
    ends.update({i: AHEAD for i in range(n) if ops[i]["q"] == "g"})
    if not MODEL:
        ids, seed = list(range(starts[1], starts[2] + 1)), [1]

        def chance():
            seed[0] = (seed[0] * 1103515245 + 12345) % 2 ** 31
            return seed[0] / 2 ** 31
        best = cur = settle({i: -tail[i] for i in ids}, 1)
        for k in range(TRIES):
            due = dict(cur[1])
            for _ in range(1 + int(3 * chance())): due[ids[int(len(ids) * chance())]] += 2 * (chance() + chance() + chance() - 1.5)
            new = settle(due, 1)
            if new[0] <= cur[0] + .2 * chance() * (1 - k / TRIES): cur = new
            if new[0] < best[0]: best = new
        MODEL.update({ops[i]["sig"][1:]: best[1][i] for i in ids[:-1]})
    at = settle({i: 100.0 * ops[i]["sig"][0] + MODEL.get(ops[i]["sig"][1:], 99.0) for i in range(n)}, 0)[1]
    order = sorted(range(n), key=lambda i: (at[i], i))

    clk, total, evs = {q: {} for q in list(Q) + ["x"]}, dict(arrived), {}
    for i in order:
        o, q, need = ops[i], ops[i]["q"], {}
        if q == "x":
            evs[i] = (o["ev"], {})
            continue
        for j in o["pre"]:
            if evs[j] is not None and not q == ops[j]["q"] == "p":
                (s, v), snap = evs[j]
                if clk[q].get(s, 0) < v and need.get(s, (0,))[0] < v: need[s] = (v, snap)
        items = sorted(need.items())
        for s, (v, snap) in items:
            if not any(s2 != s and sn2.get(s, 0) >= v for s2, (v2, sn2) in items): Q[q].wait_ge(T.sem[s], v)
        for s, (v, snap) in items:
            for s2, v2 in list(snap.items()) + [(s, v)]: clk[q][s2] = max(clk[q].get(s2, 0), v2)
        call = o["fn"]()
        if o["sem"] is None:
            evs[i] = None
            continue
        s = o["sem"] or QS[q]
        call.then_inc(T.sem[s], o["inc"])
        total[s] = total.get(s, 0) + o["inc"]
        evs[i] = ((s, total[s]), dict(clk[q]))
    total["ls"] = sent[0]
    for s in sorted(total):
        g.wait_ge(T.sem[s], total[s])
